import numpy as np
import ml_dtypes


def mxq(x, axis, fmt="e4m3"):
    dtype, down = {"e4m3": (ml_dtypes.float8_e4m3fn, 7), "e5m2": (ml_dtypes.float8_e5m2, 14)}[fmt]
    v = np.moveaxis(np.asarray(x, np.float32).astype(ml_dtypes.bfloat16).astype(np.float64), axis, -1)
    blocks = v.reshape(v.shape[:-1] + (-1, 32))
    amax = np.abs(blocks).max(-1, keepdims=True)
    byte = np.maximum(np.where(amax > 0, np.frexp(amax)[1] - 1 + 127, 0) - down, 1)
    scale = np.exp2(byte - 127.0)
    codes = (blocks / scale).astype(np.float32).astype(dtype).astype(np.float64)
    return np.moveaxis((codes * scale).reshape(v.shape), -1, axis)


WIDE = False


def mx_kscale(k):
    if not WIDE:
        return np.ones(k)
    levels = np.array([10, -10, 5, -5, 0])
    if k % 512:
        return np.exp2(np.random.permutation(np.resize(levels, k // 32))).repeat(32)
    a = np.empty((k // 512, 16))
    for p in range(k // 512):
        a[p, :8] = np.random.permutation(np.resize(levels, 8))
        for g in range(8):
            far = levels[np.abs(levels - a[p, g]) >= 10]
            a[p, g + 8] = far[np.random.randint(len(far))]
    return np.exp2(a.ravel()).repeat(32)


BF16 = ml_dtypes.bfloat16


def bf(x):
    return np.asarray(x, np.float32).astype(BF16)


def f64(x):
    return np.asarray(x).astype(np.float64)


E2M1 = np.array([0.0, 0.5, 1.0, 1.5, 2.0, 3.0, 4.0, 6.0, -0.0, -0.5, -1.0, -1.5, -2.0, -3.0, -4.0, -6.0])


def pack_weight(w, fmt):
    k, n = w.shape
    w = f64(bf(w)).reshape(k // 32, 32, n)
    amax = np.abs(w).max(1)
    if fmt == "e4m3":
        byte = np.frexp(amax)[1] - 1 + 127 - 7
    else:
        mant, ex = np.frexp(amax / 6.0)
        byte = np.where(mant > 0.5, ex, ex - 1) + 127
    byte = np.clip(np.where(amax > 0, byte, 1), 1, 254)
    scaled = (w * np.exp2(127.0 - byte)[:, None, :]).reshape(k, n).astype(np.float32)
    by_word = np.ascontiguousarray(scaled.reshape(k // 512, 128, 4, n).transpose(0, 1, 3, 2))
    if fmt == "e4m3":
        words = by_word.astype(ml_dtypes.float8_e4m3fn).view(np.uint8)
    else:
        c = by_word.astype(ml_dtypes.float4_e2m1fn).view(np.uint8) & 0xF
        words = c[..., 0::2] | (c[..., 1::2] << 4)
    return np.ascontiguousarray(words), np.ascontiguousarray(byte.astype(np.uint8).reshape(k // 512, 16, n))


def unpack_weight(words, scales, fmt):
    g, p, n, _ = words.shape
    if fmt == "e4m3":
        vals = np.ascontiguousarray(words).view(ml_dtypes.float8_e4m3fn).astype(np.float64)
    else:
        nib = np.empty((g, p, n, 4), np.uint8)
        nib[..., 0::2] = words & 0xF
        nib[..., 1::2] = words >> 4
        vals = E2M1[nib]
    vals = vals * np.repeat(np.exp2(scales.astype(np.float64) - 127.0), 8, axis=1)[..., None]
    return vals.transpose(0, 1, 3, 2).reshape(g * 512, n)
def pack4(w):
    words, scales = pack_weight(w, "e2m1")
    return words.reshape(words.shape[0], 128, -1), scales


def unpack4(words, scales):
    return unpack_weight(words.reshape(words.shape[0], 128, -1, 2), scales, "e2m1")


def planes(Y):
    n, m = Y.shape
    b = f64(bf(Y)).reshape(n // 32, 32, m)
    amax = np.abs(b).max(1)
    byte = np.clip(np.where(amax > 0, np.frexp(amax)[1] - 1 + 127 - 7, 1), 1, 254)
    codes = (b * np.exp2(127.0 - byte)[:, None, :]).reshape(n, m).astype(np.float32).astype(ml_dtypes.float8_e4m3fn).view(np.uint8)
    words = codes.reshape(n // 512, 128, 4, m).transpose(0, 1, 3, 2)
    return np.ascontiguousarray(words), np.ascontiguousarray(byte.astype(np.uint8).reshape(n // 512, 16, m))


C, R, K1, K2, Q = 1280, 1024, 512, 2048, 1024

OVERLAP = 3.0
SHARP = 4.0

def setup_inputs():
    s1, s2, t = mx_kscale(K1), mx_kscale(K2), mx_kscale(R)
    cand_low = np.random.randn(C, K1) * s1
    cand_high = np.random.randn(C, K2) * s2
    ref_low = np.random.randn(K1, R) * OVERLAP / np.sqrt(K1) / s1[:, None] * t
    ref_high = np.random.randn(K2, R) * OVERLAP / np.sqrt(K2) / s2[:, None] * t
    ref_high_words, ref_high_scales = pack4(ref_high)
    cand_len = np.exp(0.3 * np.random.randn(C))
    ref_len = np.exp(0.3 * np.random.randn(R))
    e = np.exp(1.2 * np.random.randn(R, Q))
    post = e / e.sum(axis=0) / t[:, None]
    spread = np.exp(0.8 * np.random.randn(Q))
    gain = SHARP * spread
    score = 0.4 * spread * np.random.randn(C, Q)
    return {"cand_low": bf(cand_low), "cand_high": bf(cand_high), "ref_low": bf(ref_low),
            "ref_high_words": ref_high_words, "ref_high_scales": ref_high_scales,
            "cand_len": bf(cand_len), "ref_len": bf(ref_len), "post": bf(post),
            "gain": bf(gain), "score": bf(score)}

def reference(cand_low, cand_high, ref_low, ref_high_words, ref_high_scales, cand_len, ref_len, post, gain, score):
    low = mxq(f64(cand_low), 1, "e4m3") @ mxq(f64(ref_low), 0, "e4m3")
    high = mxq(f64(cand_high), 1, "e4m3") @ unpack4(ref_high_words, ref_high_scales)
    S = (low + high) / (f64(cand_len)[:, None] + f64(ref_len)[None, :])
    U = mxq(S, 1, "e4m3") @ mxq(f64(post), 0, "e4m3")
    y = U * f64(gain)[None, :] + f64(score)
    Y = y.T
    words, scales = planes(Y)
    return y, words, scales

@@ -1,0 +1,456 @@
+from contextlib import ExitStack
+
+import concourse.mybir as mybir
+from concourse.masks import make_identity
+
+C, R, K1, K2, Q = 1280, 1024, 512, 2048, 1024
+FLOPS = 2 * C * R * (K1 + K2) + 2 * C * R * Q
+
+F32 = mybir.dt.float32
+BF16 = mybir.dt.bfloat16
+I32 = mybir.dt.int32
+U32 = mybir.dt.uint32
+U8 = mybir.dt.uint8
+FP8X4 = mybir.dt.float8_e4m3fn_x4
+FP4X4 = mybir.dt.float4_e2m1fn_x4
+ACT = mybir.ActivationFunctionType
+ALU = mybir.AluOpType
+
+P = 128
+NT = C // P
+BANK = 512
+U_AT = [1,2,3,4,5,6,7,8,-9,-9]
+POST_A = {1: [(("post",1,0),"V"),(("post",0,1),"S")]}
+POST_B = {0: [(("post",0,0),"V")], 1: [(("post",1,1),"V")]}
+POOL_ROUND = [0,1,2,3,4,5,6,7]
+POOL_ADD = []
+SORT_FROM = 3
+
+
+def tile_mbr_expected_overlap_k6_kernel(
+    tc, cand_low, cand_high, ref_low, ref_high_words, ref_high_scales, cand_len, ref_len, post, gain, score,
+    out_0, out_1, out_2,
+):
+    nc = tc.nc
+    with ExitStack() as ctx:
+        keep = ctx.enter_context(tc.tile_pool(name="keep", bufs=1))
+        work = ctx.enter_context(tc.tile_pool(name="work", bufs=2))
+        pacc = ctx.enter_context(tc.psum_pool(name="pacc", bufs=3))
+        ptr = ctx.enter_context(tc.psum_pool(name="ptr", bufs=5))
+        ctx.enter_context(tc.manual_schedule())
+
+        t = {}
+
+        def sb(kind, key, shape, dtype, bufs=2):
+            t[kind, key] = work.tile(shape, dtype, name=kind, tag=kind, bufs=bufs, align_bytes=64)
+            return t[kind, key]
+
+        def const(name, shape, dtype):
+            return keep.tile(shape, dtype, name=name, tag=name, align_bytes=64)
+
+        def tbank(kind, key):
+            t[kind, key] = ptr.tile([P, 4, P], F32, name="tbank", tag="tbank")
+            return t[kind, key]
+
+        def abank(kind, key):
+            t[kind, key] = pacc.tile([P, BANK], F32, name="abank", tag="abank")
+            return t[kind, key]
+
+        ident = const("ident", [P, P], F32)
+        len_pad = const("len_pad", [P, P], F32)
+        len_rows = const("len_rows", [NT, P], BF16)
+        warm = const("warm", [P, 2], F32)
+        rl_col = const("rl_col", [P, 2, 4], BF16)
+        gain_col = const("gain_col", [P, 2, 4], BF16)
+        lnrl_col = const("lnrl_col", [P, 8], F32)
+        gain_col32 = const("gain_col32", [P, 8], F32)
+        ln_cl = const("ln_cl", [P, NT], F32)
+        inv_cl = const("inv_cl", [P, NT], F32)
+        lnrl_all = const("lnrl_all", [P, R], F32)
+        gain_all = const("gain_all", [P, Q], F32)
+        rh_scales = const("rh_scales", [P, 4, R], U8)
+        rh_words = [const("rh_words%d" % h, [P, 4, 2 * BANK], U8) for h in range(2)]
+        y_scales = const("y_scales", [P, 2, C], U8)
+
+        def load_cand_high(i):
+            x = sb("cand_hi", i, [P, K2], BF16, bufs=5)
+            nc.sync.dma_start(out=x[:], in_=cand_high[i * P:(i + 1) * P, :])
+
+        def load_cand_low(i):
+            x = sb("cand_lo", i, [P, K1], BF16, bufs=5)
+            nc.sync.dma_start(out=x[:], in_=cand_low[i * P:(i + 1) * P, :])
+
+        def load_score(i):
+            x = sb("score", i, [P, Q], BF16, bufs=5)
+            nc.sync.dma_start(out=x[:], in_=score[i * P:(i + 1) * P, :])
+
+        def load_rows(key, rows, half):
+            x = sb("rows_raw", key, [P, 4, BANK], BF16, bufs=6)
+            nc.sync.dma_start(out=x[:], in_=rows.rearrange("(p j) n -> p j n", j=4)[:, :, half * BANK:(half + 1) * BANK])
+
+        def interleave_rows(key, copy):
+            x = sb("rows_il", key, [P, 4 * BANK], BF16, bufs=3)
+            copy(
+                out=x[:].rearrange("p (c i j) -> p c j i", i=4, j=4),
+                in_=t["rows_raw", key][:].rearrange("p j (c i) -> p c j i", i=4),
+            )
+
+        def quantize_rows(key):
+            codes = sb("rows_codes", key, [P, BANK], U32, bufs=6)
+            scales = sb("rows_scales", key, [P, BANK], U8, bufs=6)
+            nc.vector.quantize_mx(out=codes[:].bitcast(FP8X4), scales=scales[:], in_=t["rows_il", key][:])
+
+        def cand_sort(i):
+            x = sb("cand_sorted", i, [P, 5 * 256], F32)
+            nc.scalar.copy(
+                out=x[:, 0:1024].rearrange("c (g u p) -> c g u p", g=4, u=2),
+                in_=t["cand_hi", i][:].bitcast(F32).rearrange("c (g p u) -> c g u p", g=4, u=2),
+            )
+            nc.scalar.copy(
+                out=x[:, 1024:1280].rearrange("c (u p) -> c u p", u=2),
+                in_=t["cand_lo", i][:].bitcast(F32).rearrange("c (p u) -> c u p", u=2),
+            )
+
+        def cand_transpose(i, part):
+            groups = 2 if part < 2 else 1
+            if i >= SORT_FROM:
+                bank = tbank("cand_t", (i, part))
+                for j in range(2 * groups):
+                    lo = 512 * part + P * j
+                    nc.tensor.transpose(bank[:, j, :], t["cand_sorted", i][:, lo:lo + P], ident[:])
+                return
+            src = t["cand_hi", i][:].bitcast(F32) if part < 2 else t["cand_lo", i][:].bitcast(F32)
+            first = 512 * part if part < 2 else 0
+            bank = tbank("cand_t", (i, part))
+            for g in range(groups):
+                for u in range(2):
+                    lo = first + 256 * g
+                    nc.tensor.transpose(bank[:, 2 * g + u, :], src[:, lo + u:lo + 256:2], ident[:])
+
+        def pairs_out(copy, kind, key, bank, groups):
+            x = sb(kind, key, [P, groups * 4 * P], BF16, bufs=3)
+            copy(
+                out=x[:].bitcast(F32).rearrange("p (g c u) -> p g c u", g=groups, u=2),
+                in_=bank[:, 0:2 * groups, :].rearrange("p (g u) c -> p g c u", u=2),
+            )
+
+        def cand_copy(i, part, copy):
+            pairs_out(copy, "cand_k%d" % part, i, t["cand_t", (i, part)], 2 if part < 2 else 1)
+
+        def cand_quantize(i, part):
+            width = 2 * P if part < 2 else P
+            codes = sb("cand_codes%d" % part, i, [P, width], U32)
+            scales = sb("cand_scales%d" % part, i, [P, width], U8)
+            nc.vector.quantize_mx(out=codes[:].bitcast(FP8X4), scales=scales[:], in_=t["cand_k%d" % part, i][:])
+
+        def overlap_high(i, h):
+            acc = abank("O", (i, h))
+            for g in range(4):
+                cols = slice((g % 2) * P, (g % 2 + 1) * P)
+                nc.tensor.matmul_mx(
+                    out=acc[:],
+                    lhsT=t["cand_codes%d" % (g // 2), i][:, cols].bitcast(FP8X4),
+                    lhsT_scale=t["cand_scales%d" % (g // 2), i][:, cols],
+                    rhs=rh_words[h][:, g, :].bitcast(FP4X4),
+                    rhs_scale=rh_scales[:, g, h * BANK:(h + 1) * BANK],
+                    start=(g == 0), stop=False,
+                )
+
+        def overlap_low(i, h):
+            nc.tensor.matmul_mx(
+                out=t["O", (i, h)][:],
+                lhsT=t["cand_codes2", i][:].bitcast(FP8X4),
+                lhsT_scale=t["cand_scales2", i][:],
+                rhs=t["rows_codes", ("ref", h)][:].bitcast(FP8X4),
+                rhs_scale=t["rows_scales", ("ref", h)][:],
+                start=False, stop=True,
+            )
+
+        def share(i):
+            x = sb("share", i, [P, R], F32)
+            nc.scalar.activation(out=x[:], in_=lnrl_all[:], func=ACT.Sigmoid, bias=ln_cl[:, i:i + 1], scale=-1.0)
+
+        def normalise(i, h):
+            if h == 0:
+                sb("S", i, [P, R], BF16)
+            for u in range(2):
+                cols = slice(h * BANK + u * 256, h * BANK + (u + 1) * 256)
+                nc.vector.scalar_tensor_tensor(
+                    out=t["S", i][:, cols].rearrange("c (p e) -> c p e", e=2),
+                    in0=t["O", (i, h)][:].rearrange("c (p u e) -> c u p e", u=2, e=2)[:, u, :, :],
+                    scalar=inv_cl[:, i:i + 1],
+                    in1=t["share", i][:, cols].rearrange("c (p e) -> c p e", e=2),
+                    op0=ALU.mult, op1=ALU.mult,
+                )
+
+        def pairs_transpose(kind, i):
+            words = t[kind, i][:].bitcast(F32)
+            bank = tbank(kind + "_t", i)
+            for j in range(4):
+                nc.tensor.transpose(bank[:, j, :], words[:, j * P:(j + 1) * P], ident[:])
+
+        def s_quantize(i):
+            codes = sb("S_codes", i, [P, 2 * P], U32, bufs=4)
+            scales = sb("S_scales", i, [P, 2 * P], U8, bufs=4)
+            nc.vector.quantize_mx(out=codes[:].bitcast(FP8X4), scales=scales[:], in_=t["S_k", i][:])
+
+        def expected(i, half):
+            acc = abank("U", (i, half))
+            for h in range(2):
+                nc.tensor.matmul_mx(
+                    out=acc[:],
+                    lhsT=t["S_codes", i][:, h * P:(h + 1) * P].bitcast(FP8X4),
+                    lhsT_scale=t["S_scales", i][:, h * P:(h + 1) * P],
+                    rhs=t["rows_codes", ("post", h, half)][:].bitcast(FP8X4),
+                    rhs_scale=t["rows_scales", ("post", h, half)][:],
+                    start=(h == 0), stop=(h == 1),
+                )
+
+        def apply_gain(i, half):
+            if half == 0:
+                sb("scaled", i, [P, Q], F32, bufs=3)
+            cols = slice(half * BANK, (half + 1) * BANK)
+            nc.vector.tensor_tensor(out=t["scaled", i][:, cols], in0=t["U", (i, half)][:], in1=gain_all[:, cols], op=ALU.mult)
+
+        def add_score(i):
+            y = sb("y", i, [P, Q], F32, bufs=4)
+            if i in POOL_ADD:
+                for half in range(2):
+                    cols = slice(half * BANK, (half + 1) * BANK)
+                    nc.gpsimd.tensor_tensor(out=y[:, cols], in0=t["scaled", i][:, cols], in1=t["score", i][:, cols], op=ALU.add)
+            else:
+                nc.vector.tensor_tensor(out=y[:], in0=t["scaled", i][:], in1=t["score", i][:], op=ALU.add)
+            nc.sync.dma_start(out=out_0[i * P:(i + 1) * P, :], in_=y[:])
+
+        def y_round(i):
+            x = sb("Y", i, [P, Q], BF16, bufs=3)
+            if i in POOL_ROUND:
+                for g in range(2):
+                    cols = slice(g * BANK, (g + 1) * BANK)
+                    nc.gpsimd.tensor_scalar(
+                        out=x[:, cols].rearrange("c (u p e) -> c u p e", u=2, e=2),
+                        in0=t["y", i][:, cols].rearrange("c (p u e) -> c u p e", u=2, e=2),
+                        scalar1=1.0, scalar2=0.0, op0=ALU.mult, op1=ALU.add,
+                    )
+            else:
+                nc.scalar.copy(
+                    out=x[:].rearrange("c (g u p e) -> c g u p e", g=2, u=2, e=2),
+                    in_=t["y", i][:].rearrange("c (g p u e) -> c g u p e", g=2, u=2, e=2),
+                )
+
+        words_out = out_1.rearrange("g p m t -> p g (m t)").bitcast(I32)
+
+        def y_quantize(i):
+            if i % 2 == 0:
+                sb("y_codes", i // 2, [P, 2, 2 * P], U32, bufs=3)
+            codes = t["y_codes", i // 2]
+            for g in range(2):
+                nc.vector.quantize_mx(
+                    out=codes[:, g, (i % 2) * P:(i % 2 + 1) * P].bitcast(FP8X4),
+                    scales=y_scales[:, g, i * P:(i + 1) * P],
+                    in_=t["Y_k", i][:, g * BANK:(g + 1) * BANK],
+                )
+            if i % 2 == 1:
+                nc.sync.dma_start(out=words_out[:, :, (i - 1) * P:(i + 1) * P], in_=codes[:].bitcast(I32))
+
+        def last_tile(i):
+            y = sb("y", i, [P, Q], F32, bufs=4)
+            x = sb("Y", i, [P, Q], BF16, bufs=3)
+            turned = sb("Y_k", i, [P, 2 * 4 * P], BF16, bufs=3)
+            for g in range(2):
+                cols = slice(g * BANK, (g + 1) * BANK)
+                nc.vector.tensor_tensor(out=y[:, cols], in0=t["scaled", i][:, cols], in1=t["score", i][:, cols], op=ALU.add)
+                nc.sync.dma_start(out=out_0[i * P:(i + 1) * P, cols], in_=y[:, cols])
+                nc.scalar.copy(
+                    out=x[:, cols].rearrange("c (u p e) -> c u p e", u=2, e=2),
+                    in_=y[:, cols].rearrange("c (p u e) -> c u p e", u=2, e=2),
+                )
+            y_quantize(i - 1)
+            codes = t["y_codes", i // 2]
+            for g in range(2):
+                cols = slice(g * BANK, (g + 1) * BANK)
+                bank = tbank("Y_t", (i, g))
+                for u in range(2):
+                    lo = (2 * g + u) * P
+                    nc.tensor.transpose(bank[:, u, :], x[:].bitcast(F32)[:, lo:lo + P], ident[:])
+                nc.vector.tensor_copy(
+                    out=turned[:, cols].bitcast(F32).rearrange("p (c u) -> p c u", u=2),
+                    in_=bank[:, 0:2, :].rearrange("p u c -> p c u"),
+                )
+            for g in range(2):
+                nc.vector.quantize_mx(
+                    out=codes[:, g, P:2 * P].bitcast(FP8X4),
+                    scales=y_scales[:, g, i * P:(i + 1) * P],
+                    in_=turned[:, g * BANK:(g + 1) * BANK],
+                )
+            nc.sync.dma_start(out=words_out[:, :, (i - 1) * P:(i + 1) * P], in_=codes[:].bitcast(I32))
+
+        def spread(col, name):
+            for h in range(2):
+                bank = tbank(name, h)
+                for j in range(4):
+                    nc.tensor.transpose(bank[:, j, :], col[:, 4 * h + j:4 * h + j + 1].to_broadcast([P, P]), ident[:])
+
+        nc.vector.memset(rh_scales[:].rearrange("p g n -> p (g n)").bitcast(I32), 0)
+        nc.vector.memset(len_pad[:], 1.0)
+        nc.gpsimd.dma_start(out=rl_col[:], in_=ref_len.rearrange("(h p j) -> p h j", h=2, j=4))
+        nc.gpsimd.dma_start(out=len_rows[:], in_=cand_len.rearrange("(i p) -> i p", p=P))
+        make_identity(nc, ident[:])
+        nc.scalar.activation(out=warm[:, 0:1], in_=len_pad[:, P - 1:P], func=ACT.Ln)
+        nc.gpsimd.dma_start(out=gain_col[:], in_=gain.rearrange("(h p j) -> p h j", h=2, j=4))
+
+        def load_ref_high(h):
+            nc.sync.dma_start(out=rh_words[h][:].bitcast(I32), in_=word_rows[:, :, h * 2 * BANK:(h + 1) * 2 * BANK].bitcast(I32))
+
+        scale_rows = ref_high_scales.rearrange("g q n -> q g n").bitcast(I32)
+        word_rows = ref_high_words.rearrange("g p b -> p g b")
+        load_rows(("ref", 0), ref_low, 0)
+        load_cand_high(0)
+        load_cand_low(0)
+        load_rows(("ref", 1), ref_low, 1)
+        for quad in range(4):
+            nc.sync.dma_start(out=rh_scales[32 * quad:32 * quad + 4, :, :].bitcast(I32), in_=scale_rows[4 * quad:4 * quad + 4, :, :])
+        load_ref_high(0)
+        load_ref_high(1)
+        load_cand_high(1)
+        load_cand_low(1)
+        load_rows(("post", 0, 0), post[0 * BANK:1 * BANK, :], 0)
+        load_rows(("post", 1, 0), post[1 * BANK:2 * BANK, :], 0)
+        load_rows(("post", 0, 1), post[0 * BANK:1 * BANK, :], 1)
+        load_rows(("post", 1, 1), post[1 * BANK:2 * BANK, :], 1)
+        load_cand_high(2)
+        load_cand_low(2)
+        load_cand_high(3)
+        load_cand_low(3)
+        nc.scalar.activation(out=lnrl_col[:], in_=rl_col[:].rearrange("p h j -> p (h j)"), func=ACT.Ln)
+        nc.scalar.copy(out=len_pad[0:NT, :], in_=len_rows[:])
+        spread(lnrl_col, "lnrl_t")
+        len_t = tbank("len_t", 0)
+        nc.tensor.transpose(len_t[:, 0, :], len_pad[:], ident[:])
+        for h in range(2):
+            nc.scalar.copy(
+                out=lnrl_all[:, h * BANK:(h + 1) * BANK].rearrange("c (u p e) -> c u p e", u=2, e=2),
+                in_=t["lnrl_t", h][:].rearrange("c (u e) p -> c u p e", e=2),
+            )
+        nc.scalar.activation(out=ln_cl[:], in_=len_t[:, 0, 0:NT], func=ACT.Ln)
+        nc.scalar.activation(out=warm[:, 1:2], in_=ln_cl[:, 0:1], func=ACT.Sigmoid)
+        interleave_rows(("ref", 0), nc.vector.tensor_copy)
+        nc.vector.reciprocal(out=inv_cl[:], in_=len_t[:, 0, 0:NT])
+        quantize_rows(("ref", 0))
+        nc.vector.tensor_copy(out=gain_col32[:], in_=gain_col[:].rearrange("p h j -> p (h j)"))
+        for part in range(3):
+            cand_transpose(0, part)
+            cand_copy(0, part, nc.scalar.copy)
+        interleave_rows(("ref", 1), nc.vector.tensor_copy)
+        cand_quantize(0, 0)
+        cand_quantize(0, 1)
+        quantize_rows(("ref", 1))
+        cand_quantize(0, 2)
+        share(0)
+
+        def live(i):
+            return 0 <= i < NT
+
+        def second(n):
+            return [k for k in range(NT) if U_AT[k] == n]
+
+        def post_copy(keys):
+            for key, eng in keys:
+                interleave_rows(key, nc.vector.tensor_copy if eng == "V" else nc.scalar.copy)
+
+        def post_quantize(keys):
+            for key, eng in keys:
+                quantize_rows(key)
+
+        def turn_y(k):
+            pairs_transpose("Y", k)
+            pairs_out(nc.scalar.copy, "Y_k", k, t["Y_t", k], 2)
+
+        last = NT - 1
+        for n in range(NT):
+            for k in second(n + 1):
+                load_score(k)
+            if n == last - 2:
+                load_score(last - 1)
+                load_score(last)
+            overlap_high(n, 0)
+            overlap_low(n, 0)
+            for k in second(n - 1)[-1:]:
+                apply_gain(k, 1)
+            if live(n - 1):
+                pairs_out(nc.scalar.copy, "S_k", n - 1, t["S_t", n - 1], 2)
+            if live(n + 1) and n + 1 >= SORT_FROM:
+                cand_sort(n + 1)
+            post_copy(POST_A.get(n, []))
+            if live(n - 1):
+                s_quantize(n - 1)
+            post_quantize(POST_A.get(n, []))
+            for k in second(n - 1)[0:1]:
+                add_score(k)
+                y_round(k)
+            if live(n + 4):
+                load_cand_high(n + 4)
+                load_cand_low(n + 4)
+            if n == last:
+                expected(last - 1, 0)
+                expected(last - 1, 1)
+            overlap_high(n, 1)
+            overlap_low(n, 1)
+            normalise(n, 0)
+            if n == last:
+                apply_gain(last - 1, 0)
+                apply_gain(last - 1, 1)
+            if live(n + 1):
+                share(n + 1)
+            normalise(n, 1)
+            for k in second(n - 1)[1:]:
+                add_score(k)
+                y_round(k)
+            post_copy(POST_B.get(n, []))
+            if n < last:
+                for k in second(n - 3):
+                    y_quantize(k)
+            if live(n + 1):
+                for part in range(3):
+                    cand_transpose(n + 1, part)
+                    cand_copy(n + 1, part, nc.scalar.copy)
+                    cand_quantize(n + 1, part)
+            post_quantize(POST_B.get(n, []))
+            if n == 0:
+                spread(gain_col32, "gain_t")
+                for h in range(2):
+                    nc.scalar.copy(
+                        out=gain_all[:, h * BANK:(h + 1) * BANK].rearrange("c (p j) -> c p j", j=4),
+                        in_=t["gain_t", h][:].rearrange("c j p -> c p j"),
+                    )
+            if n < last:
+                for k in second(n - 2):
+                    turn_y(k)
+                pairs_transpose("S", n)
+                for k in second(n):
+                    expected(k, 0)
+                    expected(k, 1)
+                    apply_gain(k, 0)
+                    if k != second(n)[-1]:
+                        apply_gain(k, 1)
+
+        turn_y(last - 3)
+        pairs_transpose("S", last)
+        pairs_out(nc.scalar.copy, "S_k", last, t["S_t", last], 2)
+        add_score(last - 1)
+        turn_y(last - 2)
+        s_quantize(last)
+        y_round(last - 1)
+        y_quantize(last - 4)
+        expected(last, 0)
+        expected(last, 1)
+        y_quantize(last - 3)
+        y_quantize(last - 2)
+        turn_y(last - 1)
+        apply_gain(last, 0)
+        apply_gain(last, 1)
+        last_tile(last)
+
+        scale_out = out_2.rearrange("g q m -> q g m").bitcast(I32)
+        for quad in range(4):
+            nc.sync.dma_start(out=scale_out[4 * quad:4 * quad + 4, :, :], in_=y_scales[32 * quad:32 * quad + 4, :, :].bitcast(I32))

@@ -19,12 +19,12 @@ ALU = mybir.AluOpType
 P = 128
 NT = C // P
 BANK = 512
+SORT_V = [0,1]
+SORT_S = [2]
 U_AT = [1,2,3,4,5,6,7,8,-9,-9]
-POST_A = {1: [(("post",1,0),"V"),(("post",0,1),"S")]}
-POST_B = {0: [(("post",0,0),"V")], 1: [(("post",1,1),"V")]}
-POOL_ROUND = [0,1,2,3,4,5,6,7]
+POOL_ROUND = []
 POOL_ADD = []
-SORT_FROM = 3
+SORT_FROM = 4
 
 
 def tile_mbr_expected_overlap_k6_kernel(
@@ -100,24 +100,22 @@ def tile_mbr_expected_overlap_k6_kernel(
             scales = sb("rows_scales", key, [P, BANK], U8, bufs=6)
             nc.vector.quantize_mx(out=codes[:].bitcast(FP8X4), scales=scales[:], in_=t["rows_il", key][:])
 
-        def cand_sort(i):
-            x = sb("cand_sorted", i, [P, 5 * 256], F32)
-            nc.scalar.copy(
-                out=x[:, 0:1024].rearrange("c (g u p) -> c g u p", g=4, u=2),
-                in_=t["cand_hi", i][:].bitcast(F32).rearrange("c (g p u) -> c g u p", g=4, u=2),
-            )
-            nc.scalar.copy(
-                out=x[:, 1024:1280].rearrange("c (u p) -> c u p", u=2),
-                in_=t["cand_lo", i][:].bitcast(F32).rearrange("c (p u) -> c u p", u=2),
-            )
+        def cand_sort(i, parts, copy):
+            for part in parts:
+                groups = 2 if part < 2 else 1
+                x = sb("cand_sorted%d" % part, i, [P, groups * 256], F32)
+                src = t["cand_hi", i][:].bitcast(F32)[:, 512 * part:512 * (part + 1)] if part < 2 else t["cand_lo", i][:].bitcast(F32)
+                copy(
+                    out=x[:].rearrange("c (g u p) -> c g u p", g=groups, u=2),
+                    in_=src.rearrange("c (g p u) -> c g u p", g=groups, u=2),
+                )
 
         def cand_transpose(i, part):
             groups = 2 if part < 2 else 1
-            if i >= SORT_FROM:
+            if i >= SORT_FROM and part in SORT_V + SORT_S:
                 bank = tbank("cand_t", (i, part))
                 for j in range(2 * groups):
-                    lo = 512 * part + P * j
-                    nc.tensor.transpose(bank[:, j, :], t["cand_sorted", i][:, lo:lo + P], ident[:])
+                    nc.tensor.transpose(bank[:, j, :], t["cand_sorted%d" % part, i][:, P * j:P * (j + 1)], ident[:])
                 return
             src = t["cand_hi", i][:].bitcast(F32) if part < 2 else t["cand_lo", i][:].bitcast(F32)
             first = 512 * part if part < 2 else 0
@@ -293,24 +291,24 @@ def tile_mbr_expected_overlap_k6_kernel(
 
         nc.vector.memset(rh_scales[:].rearrange("p g n -> p (g n)").bitcast(I32), 0)
         nc.vector.memset(len_pad[:], 1.0)
-        nc.gpsimd.dma_start(out=rl_col[:], in_=ref_len.rearrange("(h p j) -> p h j", h=2, j=4))
-        nc.gpsimd.dma_start(out=len_rows[:], in_=cand_len.rearrange("(i p) -> i p", p=P))
         make_identity(nc, ident[:])
         nc.scalar.activation(out=warm[:, 0:1], in_=len_pad[:, P - 1:P], func=ACT.Ln)
-        nc.gpsimd.dma_start(out=gain_col[:], in_=gain.rearrange("(h p j) -> p h j", h=2, j=4))
 
         def load_ref_high(h):
             nc.sync.dma_start(out=rh_words[h][:].bitcast(I32), in_=word_rows[:, :, h * 2 * BANK:(h + 1) * 2 * BANK].bitcast(I32))
 
         scale_rows = ref_high_scales.rearrange("g q n -> q g n").bitcast(I32)
         word_rows = ref_high_words.rearrange("g p b -> p g b")
+        nc.sync.dma_start(out=rl_col[:], in_=ref_len.rearrange("(h p j) -> p h j", h=2, j=4))
+        nc.sync.dma_start(out=len_rows[:], in_=cand_len.rearrange("(i p) -> i p", p=P))
+        nc.sync.dma_start(out=gain_col[:], in_=gain.rearrange("(h p j) -> p h j", h=2, j=4))
         load_rows(("ref", 0), ref_low, 0)
         load_cand_high(0)
         load_cand_low(0)
-        load_rows(("ref", 1), ref_low, 1)
+        load_ref_high(0)
         for quad in range(4):
             nc.sync.dma_start(out=rh_scales[32 * quad:32 * quad + 4, :, :].bitcast(I32), in_=scale_rows[4 * quad:4 * quad + 4, :, :])
-        load_ref_high(0)
+        load_rows(("ref", 1), ref_low, 1)
         load_ref_high(1)
         load_cand_high(1)
         load_cand_low(1)
@@ -323,44 +321,40 @@ def tile_mbr_expected_overlap_k6_kernel(
         load_cand_high(3)
         load_cand_low(3)
         nc.scalar.activation(out=lnrl_col[:], in_=rl_col[:].rearrange("p h j -> p (h j)"), func=ACT.Ln)
-        nc.scalar.copy(out=len_pad[0:NT, :], in_=len_rows[:])
-        spread(lnrl_col, "lnrl_t")
+        nc.vector.tensor_copy(out=len_pad[0:NT, :], in_=len_rows[:])
+        nc.vector.tensor_copy(out=gain_col32[:], in_=gain_col[:].rearrange("p h j -> p (h j)"))
         len_t = tbank("len_t", 0)
         nc.tensor.transpose(len_t[:, 0, :], len_pad[:], ident[:])
+        spread(lnrl_col, "lnrl_t")
+        spread(gain_col32, "gain_t")
+        nc.scalar.activation(out=ln_cl[:], in_=len_t[:, 0, 0:NT], func=ACT.Ln)
+        nc.vector.reciprocal(out=inv_cl[:], in_=len_t[:, 0, 0:NT])
+        nc.scalar.activation(out=warm[:, 1:2], in_=ln_cl[:, 0:1], func=ACT.Sigmoid)
         for h in range(2):
             nc.scalar.copy(
                 out=lnrl_all[:, h * BANK:(h + 1) * BANK].rearrange("c (u p e) -> c u p e", u=2, e=2),
                 in_=t["lnrl_t", h][:].rearrange("c (u e) p -> c u p e", e=2),
             )
-        nc.scalar.activation(out=ln_cl[:], in_=len_t[:, 0, 0:NT], func=ACT.Ln)
-        nc.scalar.activation(out=warm[:, 1:2], in_=ln_cl[:, 0:1], func=ACT.Sigmoid)
         interleave_rows(("ref", 0), nc.vector.tensor_copy)
-        nc.vector.reciprocal(out=inv_cl[:], in_=len_t[:, 0, 0:NT])
         quantize_rows(("ref", 0))
-        nc.vector.tensor_copy(out=gain_col32[:], in_=gain_col[:].rearrange("p h j -> p (h j)"))
         for part in range(3):
             cand_transpose(0, part)
             cand_copy(0, part, nc.scalar.copy)
+            cand_quantize(0, part)
         interleave_rows(("ref", 1), nc.vector.tensor_copy)
-        cand_quantize(0, 0)
-        cand_quantize(0, 1)
-        quantize_rows(("ref", 1))
-        cand_quantize(0, 2)
         share(0)
+        quantize_rows(("ref", 1))
+        for h in range(2):
+            nc.scalar.copy(
+                out=gain_all[:, h * BANK:(h + 1) * BANK].rearrange("c (p j) -> c p j", j=4),
+                in_=t["gain_t", h][:].rearrange("c j p -> c p j"),
+            )
 
         def live(i):
             return 0 <= i < NT
 
         def second(n):
             return [k for k in range(NT) if U_AT[k] == n]
-
-        def post_copy(keys):
-            for key, eng in keys:
-                interleave_rows(key, nc.vector.tensor_copy if eng == "V" else nc.scalar.copy)
-
-        def post_quantize(keys):
-            for key, eng in keys:
-                quantize_rows(key)
 
         def turn_y(k):
             pairs_transpose("Y", k)
@@ -375,19 +369,29 @@ def tile_mbr_expected_overlap_k6_kernel(
                 load_score(last)
             overlap_high(n, 0)
             overlap_low(n, 0)
-            for k in second(n - 1)[-1:]:
-                apply_gain(k, 1)
+            if n > 2:
+                apply_gain(n - 2, 1)
             if live(n - 1):
                 pairs_out(nc.scalar.copy, "S_k", n - 1, t["S_t", n - 1], 2)
+            for k in second(n - 2):
+                y_round(k)
             if live(n + 1) and n + 1 >= SORT_FROM:
-                cand_sort(n + 1)
-            post_copy(POST_A.get(n, []))
+                cand_sort(n + 1, SORT_S, nc.scalar.copy)
+            if n == 1:
+                interleave_rows(("post", 0, 0), nc.vector.tensor_copy)
+                interleave_rows(("post", 1, 0), nc.scalar.copy)
+            if n == 2:
+                interleave_rows(("post", 1, 1), nc.scalar.copy)
             if live(n - 1):
                 s_quantize(n - 1)
-            post_quantize(POST_A.get(n, []))
-            for k in second(n - 1)[0:1]:
-                add_score(k)
-                y_round(k)
+            if n == 1:
+                quantize_rows(("post", 0, 0))
+            if n == 2:
+                quantize_rows(("post", 0, 1))
+            if live(n + 1) and n + 1 >= SORT_FROM:
+                cand_sort(n + 1, SORT_V, nc.vector.tensor_copy)
+            if n > 2:
+                add_score(n - 2)
             if live(n + 4):
                 load_cand_high(n + 4)
                 load_cand_low(n + 4)
@@ -397,16 +401,19 @@ def tile_mbr_expected_overlap_k6_kernel(
             overlap_high(n, 1)
             overlap_low(n, 1)
             normalise(n, 0)
+            if n == 2:
+                quantize_rows(("post", 1, 1))
+                expected(0, 1)
             if n == last:
                 apply_gain(last - 1, 0)
                 apply_gain(last - 1, 1)
             if live(n + 1):
                 share(n + 1)
             normalise(n, 1)
-            for k in second(n - 1)[1:]:
-                add_score(k)
-                y_round(k)
-            post_copy(POST_B.get(n, []))
+            if n == 2:
+                apply_gain(0, 1)
+            if n == 1:
+                quantize_rows(("post", 1, 0))
             if n < last:
                 for k in second(n - 3):
                     y_quantize(k)
@@ -415,25 +422,21 @@ def tile_mbr_expected_overlap_k6_kernel(
                     cand_transpose(n + 1, part)
                     cand_copy(n + 1, part, nc.scalar.copy)
                     cand_quantize(n + 1, part)
-            post_quantize(POST_B.get(n, []))
-            if n == 0:
-                spread(gain_col32, "gain_t")
-                for h in range(2):
-                    nc.scalar.copy(
-                        out=gain_all[:, h * BANK:(h + 1) * BANK].rearrange("c (p j) -> c p j", j=4),
-                        in_=t["gain_t", h][:].rearrange("c j p -> c p j"),
-                    )
+            if n == 1:
+                interleave_rows(("post", 0, 1), nc.vector.tensor_copy)
+            if n == 2:
+                add_score(0)
             if n < last:
                 for k in second(n - 2):
                     turn_y(k)
                 pairs_transpose("S", n)
                 for k in second(n):
                     expected(k, 0)
-                    expected(k, 1)
+                    if k > 0:
+                        expected(k, 1)
                     apply_gain(k, 0)
-                    if k != second(n)[-1]:
-                        apply_gain(k, 1)
 
+        y_round(last - 2)
         turn_y(last - 3)
         pairs_transpose("S", last)
         pairs_out(nc.scalar.copy, "S_k", last, t["S_t", last], 2)

@@ -19,11 +19,8 @@ ALU = mybir.AluOpType
 P = 128
 NT = C // P
 BANK = 512
-SORT_V = [0,1]
-SORT_S = [2]
-U_AT = [1,2,3,4,5,6,7,8,-9,-9]
-POOL_ROUND = []
-POOL_ADD = []
+POOL_UNTIL = 7
+POST_PLAN = {(0,2): [((0,0),"V"),((0,1),"S")], (0,3): [((0,0),"Q")], (1,0): [((0,1),"Q")], (1,1): [((1,0),"V")], (1,2): [((1,1),"S"),((1,0),"Q")], (2,0): [((1,1),"Q")]}
 SORT_FROM = 4
 
 
@@ -35,8 +32,7 @@ def tile_mbr_expected_overlap_k6_kernel(
     with ExitStack() as ctx:
         keep = ctx.enter_context(tc.tile_pool(name="keep", bufs=1))
         work = ctx.enter_context(tc.tile_pool(name="work", bufs=2))
-        pacc = ctx.enter_context(tc.psum_pool(name="pacc", bufs=3))
-        ptr = ctx.enter_context(tc.psum_pool(name="ptr", bufs=5))
+        psum = ctx.enter_context(tc.psum_pool(name="psum", bufs=8))
         ctx.enter_context(tc.manual_schedule())
 
         t = {}
@@ -49,11 +45,11 @@ def tile_mbr_expected_overlap_k6_kernel(
             return keep.tile(shape, dtype, name=name, tag=name, align_bytes=64)
 
         def tbank(kind, key):
-            t[kind, key] = ptr.tile([P, 4, P], F32, name="tbank", tag="tbank")
+            t[kind, key] = psum.tile([P, 4, P], F32, name="bank", tag="bank")
             return t[kind, key]
 
         def abank(kind, key):
-            t[kind, key] = pacc.tile([P, BANK], F32, name="abank", tag="abank")
+            t[kind, key] = psum.tile([P, BANK], F32, name="bank", tag="bank")
             return t[kind, key]
 
         ident = const("ident", [P, P], F32)
@@ -84,15 +80,22 @@ def tile_mbr_expected_overlap_k6_kernel(
             x = sb("score", i, [P, Q], BF16, bufs=5)
             nc.sync.dma_start(out=x[:], in_=score[i * P:(i + 1) * P, :])
 
-        def load_rows(key, rows, half):
-            x = sb("rows_raw", key, [P, 4, BANK], BF16, bufs=6)
-            nc.sync.dma_start(out=x[:], in_=rows.rearrange("(p j) n -> p j n", j=4)[:, :, half * BANK:(half + 1) * BANK])
+        def load_ref_low(h):
+            x = sb("ref_raw", h, [P, 4, BANK], BF16)
+            nc.sync.dma_start(out=x[:], in_=ref_low.rearrange("(p j) n -> p j n", j=4)[:, :, h * BANK:(h + 1) * BANK])
+            t["rows_raw", ("ref", h)] = x[:]
+
+        def load_post(h):
+            x = sb("post_raw", h, [P, 4, Q], BF16)
+            nc.sync.dma_start(out=x[:], in_=post[h * BANK:(h + 1) * BANK, :].rearrange("(p j) n -> p j n", j=4))
+            for half in range(2):
+                t["rows_raw", ("post", h, half)] = x[:, :, half * BANK:(half + 1) * BANK]
 
         def interleave_rows(key, copy):
             x = sb("rows_il", key, [P, 4 * BANK], BF16, bufs=3)
             copy(
                 out=x[:].rearrange("p (c i j) -> p c j i", i=4, j=4),
-                in_=t["rows_raw", key][:].rearrange("p j (c i) -> p c j i", i=4),
+                in_=t["rows_raw", key].rearrange("p j (c i) -> p c j i", i=4),
             )
 
         def quantize_rows(key):
@@ -100,55 +103,62 @@ def tile_mbr_expected_overlap_k6_kernel(
             scales = sb("rows_scales", key, [P, BANK], U8, bufs=6)
             nc.vector.quantize_mx(out=codes[:].bitcast(FP8X4), scales=scales[:], in_=t["rows_il", key][:])
 
-        def cand_sort(i, parts, copy):
-            for part in parts:
-                groups = 2 if part < 2 else 1
-                x = sb("cand_sorted%d" % part, i, [P, groups * 256], F32)
-                src = t["cand_hi", i][:].bitcast(F32)[:, 512 * part:512 * (part + 1)] if part < 2 else t["cand_lo", i][:].bitcast(F32)
-                copy(
-                    out=x[:].rearrange("c (g u p) -> c g u p", g=groups, u=2),
-                    in_=src.rearrange("c (g p u) -> c g u p", g=groups, u=2),
-                )
+        def cand_sort(i, kind, copy):
+            groups = 4 if kind == "hi" else 1
+            x = sb("cand_sorted_" + kind, i, [P, groups * 256], F32)
+            copy(
+                out=x[:].rearrange("c (g u p) -> c g u p", g=groups, u=2),
+                in_=t["cand_" + kind, i][:].bitcast(F32).rearrange("c (g p u) -> c g u p", g=groups, u=2),
+            )
 
         def cand_transpose(i, part):
             groups = 2 if part < 2 else 1
-            if i >= SORT_FROM and part in SORT_V + SORT_S:
-                bank = tbank("cand_t", (i, part))
-                for j in range(2 * groups):
-                    nc.tensor.transpose(bank[:, j, :], t["cand_sorted%d" % part, i][:, P * j:P * (j + 1)], ident[:])
-                return
-            src = t["cand_hi", i][:].bitcast(F32) if part < 2 else t["cand_lo", i][:].bitcast(F32)
+            kind = "hi" if part < 2 else "lo"
             first = 512 * part if part < 2 else 0
             bank = tbank("cand_t", (i, part))
             for g in range(groups):
                 for u in range(2):
                     lo = first + 256 * g
-                    nc.tensor.transpose(bank[:, 2 * g + u, :], src[:, lo + u:lo + 256:2], ident[:])
+                    if i >= SORT_FROM:
+                        src = t["cand_sorted_" + kind, i][:, lo + P * u:lo + P * (u + 1)]
+                    else:
+                        src = t["cand_" + kind, i][:].bitcast(F32)[:, lo + u:lo + 256:2]
+                    nc.tensor.transpose(bank[:, 2 * g + u, :], src, ident[:])
 
-        def pairs_out(copy, kind, key, bank, groups):
-            x = sb(kind, key, [P, groups * 4 * P], BF16, bufs=3)
+        def pairs_out(copy, x, bank, groups):
             copy(
-                out=x[:].bitcast(F32).rearrange("p (g c u) -> p g c u", g=groups, u=2),
+                out=x.bitcast(F32).rearrange("p (g c u) -> p g c u", g=groups, u=2),
                 in_=bank[:, 0:2 * groups, :].rearrange("p (g u) c -> p g c u", u=2),
             )
 
-        def cand_copy(i, part, copy):
-            pairs_out(copy, "cand_k%d" % part, i, t["cand_t", (i, part)], 2 if part < 2 else 1)
+        def cand_copy(i, part, copy=nc.scalar.copy):
+            if part == 0:
+                sb("cand_k_hi", i, [P, K2], BF16)
+            if part == 2:
+                sb("cand_k_lo", i, [P, K1], BF16)
+                pairs_out(nc.scalar.copy, t["cand_k_lo", i][:], t["cand_t", (i, part)], 1)
+            else:
+                pairs_out(copy, t["cand_k_hi", i][:, 1024 * part:1024 * (part + 1)], t["cand_t", (i, part)], 2)
 
-        def cand_quantize(i, part):
-            width = 2 * P if part < 2 else P
-            codes = sb("cand_codes%d" % part, i, [P, width], U32)
-            scales = sb("cand_scales%d" % part, i, [P, width], U8)
-            nc.vector.quantize_mx(out=codes[:].bitcast(FP8X4), scales=scales[:], in_=t["cand_k%d" % part, i][:])
+        def cand_quantize(i, kind, parts=1):
+            width = 4 * P if kind == "hi" else P
+            codes = sb("cand_codes_" + kind, i, [P, width], U32)
+            scales = sb("cand_scales_" + kind, i, [P, width], U8)
+            step = width // parts
+            for lo in range(0, width, step):
+                nc.vector.quantize_mx(
+                    out=codes[:, lo:lo + step].bitcast(FP8X4), scales=scales[:, lo:lo + step],
+                    in_=t["cand_k_" + kind, i][:, 4 * lo:4 * (lo + step)],
+                )
 
         def overlap_high(i, h):
             acc = abank("O", (i, h))
             for g in range(4):
-                cols = slice((g % 2) * P, (g % 2 + 1) * P)
+                cols = slice(g * P, (g + 1) * P)
                 nc.tensor.matmul_mx(
                     out=acc[:],
-                    lhsT=t["cand_codes%d" % (g // 2), i][:, cols].bitcast(FP8X4),
-                    lhsT_scale=t["cand_scales%d" % (g // 2), i][:, cols],
+                    lhsT=t["cand_codes_hi", i][:, cols].bitcast(FP8X4),
+                    lhsT_scale=t["cand_scales_hi", i][:, cols],
                     rhs=rh_words[h][:, g, :].bitcast(FP4X4),
                     rhs_scale=rh_scales[:, g, h * BANK:(h + 1) * BANK],
                     start=(g == 0), stop=False,
@@ -157,8 +167,8 @@ def tile_mbr_expected_overlap_k6_kernel(
         def overlap_low(i, h):
             nc.tensor.matmul_mx(
                 out=t["O", (i, h)][:],
-                lhsT=t["cand_codes2", i][:].bitcast(FP8X4),
-                lhsT_scale=t["cand_scales2", i][:],
+                lhsT=t["cand_codes_lo", i][:].bitcast(FP8X4),
+                lhsT_scale=t["cand_scales_lo", i][:],
                 rhs=t["rows_codes", ("ref", h)][:].bitcast(FP8X4),
                 rhs_scale=t["rows_scales", ("ref", h)][:],
                 start=False, stop=True,
@@ -212,17 +222,12 @@ def tile_mbr_expected_overlap_k6_kernel(
 
         def add_score(i):
             y = sb("y", i, [P, Q], F32, bufs=4)
-            if i in POOL_ADD:
-                for half in range(2):
-                    cols = slice(half * BANK, (half + 1) * BANK)
-                    nc.gpsimd.tensor_tensor(out=y[:, cols], in0=t["scaled", i][:, cols], in1=t["score", i][:, cols], op=ALU.add)
-            else:
-                nc.vector.tensor_tensor(out=y[:], in0=t["scaled", i][:], in1=t["score", i][:], op=ALU.add)
+            nc.vector.tensor_tensor(out=y[:], in0=t["scaled", i][:], in1=t["score", i][:], op=ALU.add)
             nc.sync.dma_start(out=out_0[i * P:(i + 1) * P, :], in_=y[:])
 
         def y_round(i):
             x = sb("Y", i, [P, Q], BF16, bufs=3)
-            if i in POOL_ROUND:
+            if 0 < i < POOL_UNTIL:
                 for g in range(2):
                     cols = slice(g * BANK, (g + 1) * BANK)
                     nc.gpsimd.tensor_scalar(
@@ -235,6 +240,10 @@ def tile_mbr_expected_overlap_k6_kernel(
                     out=x[:].rearrange("c (g u p e) -> c g u p e", g=2, u=2, e=2),
                     in_=t["y", i][:].rearrange("c (g p u e) -> c g u p e", g=2, u=2, e=2),
                 )
+
+        def turned_out(kind, i):
+            x = sb(kind + "_k", i, [P, 2 * 4 * P], BF16, bufs=3)
+            pairs_out(nc.scalar.copy, x[:], t[kind + "_t", i], 2)
 
         words_out = out_1.rearrange("g p m t -> p g (m t)").bitcast(I32)
 
@@ -251,43 +260,45 @@ def tile_mbr_expected_overlap_k6_kernel(
             if i % 2 == 1:
                 nc.sync.dma_start(out=words_out[:, :, (i - 1) * P:(i + 1) * P], in_=codes[:].bitcast(I32))
 
-        def last_tile(i):
-            y = sb("y", i, [P, Q], F32, bufs=4)
-            x = sb("Y", i, [P, Q], BF16, bufs=3)
-            turned = sb("Y_k", i, [P, 2 * 4 * P], BF16, bufs=3)
-            for g in range(2):
-                cols = slice(g * BANK, (g + 1) * BANK)
-                nc.vector.tensor_tensor(out=y[:, cols], in0=t["scaled", i][:, cols], in1=t["score", i][:, cols], op=ALU.add)
-                nc.sync.dma_start(out=out_0[i * P:(i + 1) * P, cols], in_=y[:, cols])
-                nc.scalar.copy(
-                    out=x[:, cols].rearrange("c (u p e) -> c u p e", u=2, e=2),
-                    in_=y[:, cols].rearrange("c (p u e) -> c u p e", u=2, e=2),
-                )
-            y_quantize(i - 1)
+        def half_add(i, g):
+            if g == 0:
+                sb("y", i, [P, Q], F32, bufs=4)
+            cols = slice(g * BANK, (g + 1) * BANK)
+            nc.vector.tensor_tensor(out=t["y", i][:, cols], in0=t["scaled", i][:, cols], in1=t["score", i][:, cols], op=ALU.add)
+            nc.sync.dma_start(out=out_0[i * P:(i + 1) * P, cols], in_=t["y", i][:, cols])
+
+        def half_round(i, g, copy):
+            if g == 0:
+                sb("Y", i, [P, Q], BF16, bufs=3)
+            cols = slice(g * BANK, (g + 1) * BANK)
+            copy(
+                out=t["Y", i][:, cols].rearrange("c (u p e) -> c u p e", u=2, e=2),
+                in_=t["y", i][:, cols].rearrange("c (p u e) -> c u p e", u=2, e=2),
+            )
+
+        def half_turn(i, g, copy):
+            if g == 0:
+                sb("Y_k", i, [P, 2 * 4 * P], BF16, bufs=3)
+            bank = tbank("Y_t", (i, g))
+            for u in range(2):
+                lo = (2 * g + u) * P
+                nc.tensor.transpose(bank[:, u, :], t["Y", i][:].bitcast(F32)[:, lo:lo + P], ident[:])
+            pairs_out(copy, t["Y_k", i][:, g * BANK:(g + 1) * BANK], bank, 1)
+
+        def half_quantize(i, g):
             codes = t["y_codes", i // 2]
-            for g in range(2):
-                cols = slice(g * BANK, (g + 1) * BANK)
-                bank = tbank("Y_t", (i, g))
-                for u in range(2):
-                    lo = (2 * g + u) * P
-                    nc.tensor.transpose(bank[:, u, :], x[:].bitcast(F32)[:, lo:lo + P], ident[:])
-                nc.vector.tensor_copy(
-                    out=turned[:, cols].bitcast(F32).rearrange("p (c u) -> p c u", u=2),
-                    in_=bank[:, 0:2, :].rearrange("p u c -> p c u"),
-                )
-            for g in range(2):
-                nc.vector.quantize_mx(
-                    out=codes[:, g, P:2 * P].bitcast(FP8X4),
-                    scales=y_scales[:, g, i * P:(i + 1) * P],
-                    in_=turned[:, g * BANK:(g + 1) * BANK],
-                )
-            nc.sync.dma_start(out=words_out[:, :, (i - 1) * P:(i + 1) * P], in_=codes[:].bitcast(I32))
+            nc.vector.quantize_mx(
+                out=codes[:, g, P:2 * P].bitcast(FP8X4),
+                scales=y_scales[:, g, i * P:(i + 1) * P],
+                in_=t["Y_k", i][:, g * BANK:(g + 1) * BANK],
+            )
+            nc.sync.dma_start(out=words_out[:, g, (i - 1) * P:(i + 1) * P], in_=codes[:, g, :].bitcast(I32))
 
         def spread(col, name):
             for h in range(2):
-                bank = tbank(name, h)
+                bank = abank(name, h)
                 for j in range(4):
-                    nc.tensor.transpose(bank[:, j, :], col[:, 4 * h + j:4 * h + j + 1].to_broadcast([P, P]), ident[:])
+                    nc.tensor.transpose(bank[:, j * P:(j + 1) * P], col[:, 4 * h + j:4 * h + j + 1].to_broadcast([P, P]), ident[:])
 
         nc.vector.memset(rh_scales[:].rearrange("p g n -> p (g n)").bitcast(I32), 0)
         nc.vector.memset(len_pad[:], 1.0)
@@ -302,24 +313,23 @@ def tile_mbr_expected_overlap_k6_kernel(
         nc.sync.dma_start(out=rl_col[:], in_=ref_len.rearrange("(h p j) -> p h j", h=2, j=4))
         nc.sync.dma_start(out=len_rows[:], in_=cand_len.rearrange("(i p) -> i p", p=P))
         nc.sync.dma_start(out=gain_col[:], in_=gain.rearrange("(h p j) -> p h j", h=2, j=4))
-        load_rows(("ref", 0), ref_low, 0)
+        load_ref_low(0)
         load_cand_high(0)
         load_cand_low(0)
         load_ref_high(0)
         for quad in range(4):
             nc.sync.dma_start(out=rh_scales[32 * quad:32 * quad + 4, :, :].bitcast(I32), in_=scale_rows[4 * quad:4 * quad + 4, :, :])
-        load_rows(("ref", 1), ref_low, 1)
-        load_ref_high(1)
         load_cand_high(1)
         load_cand_low(1)
-        load_rows(("post", 0, 0), post[0 * BANK:1 * BANK, :], 0)
-        load_rows(("post", 1, 0), post[1 * BANK:2 * BANK, :], 0)
-        load_rows(("post", 0, 1), post[0 * BANK:1 * BANK, :], 1)
-        load_rows(("post", 1, 1), post[1 * BANK:2 * BANK, :], 1)
+        load_ref_low(1)
+        load_ref_high(1)
+        load_post(0)
         load_cand_high(2)
         load_cand_low(2)
+        load_post(1)
         load_cand_high(3)
         load_cand_low(3)
+
         nc.scalar.activation(out=lnrl_col[:], in_=rl_col[:].rearrange("p h j -> p (h j)"), func=ACT.Ln)
         nc.vector.tensor_copy(out=len_pad[0:NT, :], in_=len_rows[:])
         nc.vector.tensor_copy(out=gain_col32[:], in_=gain_col[:].rearrange("p h j -> p (h j)"))
@@ -333,126 +343,137 @@ def tile_mbr_expected_overlap_k6_kernel(
         for h in range(2):
             nc.scalar.copy(
                 out=lnrl_all[:, h * BANK:(h + 1) * BANK].rearrange("c (u p e) -> c u p e", u=2, e=2),
-                in_=t["lnrl_t", h][:].rearrange("c (u e) p -> c u p e", e=2),
+                in_=t["lnrl_t", h][:].rearrange("c (u e p) -> c u p e", u=2, e=2),
             )
         interleave_rows(("ref", 0), nc.vector.tensor_copy)
         quantize_rows(("ref", 0))
         for part in range(3):
             cand_transpose(0, part)
-            cand_copy(0, part, nc.scalar.copy)
-            cand_quantize(0, part)
-        interleave_rows(("ref", 1), nc.vector.tensor_copy)
+            cand_copy(0, part, nc.vector.tensor_copy if part == 0 else nc.scalar.copy)
+        cand_quantize(0, "hi", parts=2)
+        cand_quantize(0, "lo")
         share(0)
-        quantize_rows(("ref", 1))
+        overlap_high(0, 0)
+        overlap_low(0, 0)
+        interleave_rows(("ref", 1), nc.vector.tensor_copy)
         for h in range(2):
             nc.scalar.copy(
                 out=gain_all[:, h * BANK:(h + 1) * BANK].rearrange("c (p j) -> c p j", j=4),
-                in_=t["gain_t", h][:].rearrange("c j p -> c p j"),
+                in_=t["gain_t", h][:].rearrange("c (j p) -> c p j", j=4),
             )
+        normalise(0, 0)
+        quantize_rows(("ref", 1))
 
         def live(i):
             return 0 <= i < NT
 
-        def second(n):
-            return [k for k in range(NT) if U_AT[k] == n]
-
-        def turn_y(k):
-            pairs_transpose("Y", k)
-            pairs_out(nc.scalar.copy, "Y_k", k, t["Y_t", k], 2)
+        def prepare_post(n, slot):
+            for key, step in POST_PLAN.get((n, slot), []):
+                if step == "Q":
+                    quantize_rows(("post",) + key)
+                else:
+                    interleave_rows(("post",) + key, nc.vector.tensor_copy if step == "V" else nc.scalar.copy)
 
         last = NT - 1
-        for n in range(NT):
-            for k in second(n + 1):
-                load_score(k)
-            if n == last - 2:
+        for n in range(last):
+            if live(n - 1):
+                load_score(n - 1)
+            if n == last - 1:
                 load_score(last - 1)
                 load_score(last)
-            overlap_high(n, 0)
-            overlap_low(n, 0)
-            if n > 2:
-                apply_gain(n - 2, 1)
-            if live(n - 1):
-                pairs_out(nc.scalar.copy, "S_k", n - 1, t["S_t", n - 1], 2)
-            for k in second(n - 2):
-                y_round(k)
-            if live(n + 1) and n + 1 >= SORT_FROM:
-                cand_sort(n + 1, SORT_S, nc.scalar.copy)
-            if n == 1:
-                interleave_rows(("post", 0, 0), nc.vector.tensor_copy)
-                interleave_rows(("post", 1, 0), nc.scalar.copy)
-            if n == 2:
-                interleave_rows(("post", 1, 1), nc.scalar.copy)
-            if live(n - 1):
-                s_quantize(n - 1)
-            if n == 1:
-                quantize_rows(("post", 0, 0))
-            if n == 2:
-                quantize_rows(("post", 0, 1))
-            if live(n + 1) and n + 1 >= SORT_FROM:
-                cand_sort(n + 1, SORT_V, nc.vector.tensor_copy)
-            if n > 2:
-                add_score(n - 2)
             if live(n + 4):
                 load_cand_high(n + 4)
                 load_cand_low(n + 4)
-            if n == last:
-                expected(last - 1, 0)
-                expected(last - 1, 1)
-            overlap_high(n, 1)
-            overlap_low(n, 1)
-            normalise(n, 0)
-            if n == 2:
-                quantize_rows(("post", 1, 1))
-                expected(0, 1)
-            if n == last:
-                apply_gain(last - 1, 0)
-                apply_gain(last - 1, 1)
-            if live(n + 1):
-                share(n + 1)
-            normalise(n, 1)
-            if n == 2:
-                apply_gain(0, 1)
-            if n == 1:
-                quantize_rows(("post", 1, 0))
-            if n < last:
-                for k in second(n - 3):
-                    y_quantize(k)
+            if live(n - 1):
+                pairs_transpose("S", n - 1)
+                turned_out("S", n - 1)
             if live(n + 1):
                 for part in range(3):
                     cand_transpose(n + 1, part)
-                    cand_copy(n + 1, part, nc.scalar.copy)
-                    cand_quantize(n + 1, part)
-            if n == 1:
-                interleave_rows(("post", 0, 1), nc.vector.tensor_copy)
+                    cand_copy(n + 1, part)
+            for k in ([n - 4] if n >= 4 else []):
+                pairs_transpose("Y", k)
+                turned_out("Y", k)
+            prepare_post(n, 0)
+            if live(n - 1):
+                s_quantize(n - 1)
+            for k in ([n - 5] if n >= 5 else []):
+                y_quantize(k)
+            if live(n + 2) and n + 2 >= SORT_FROM:
+                cand_sort(n + 2, "lo", nc.vector.tensor_copy)
+            if live(n + 1):
+                cand_quantize(n + 1, "hi", parts=2)
+                cand_quantize(n + 1, "lo")
+            prepare_post(n, 1)
+            if live(n + 1):
+                share(n + 1)
+            if live(n + 2) and n + 2 >= SORT_FROM:
+                cand_sort(n + 2, "hi", nc.scalar.copy)
+            if n == 3:
+                y_round(0)
+            if n >= 3:
+                add_score(n - 2)
+                y_round(n - 2)
+            overlap_high(n, 1)
+            overlap_low(n, 1)
+            normalise(n, 1)
+            prepare_post(n, 2)
+            for k in ([] if n < 2 else [0, 1] if n == 2 else [n - 1]):
+                expected(k, 0)
+                expected(k, 1)
+                apply_gain(k, 0)
+                apply_gain(k, 1)
+            if live(n + 1):
+                overlap_high(n + 1, 0)
+                overlap_low(n + 1, 0)
             if n == 2:
                 add_score(0)
-            if n < last:
-                for k in second(n - 2):
-                    turn_y(k)
-                pairs_transpose("S", n)
-                for k in second(n):
-                    expected(k, 0)
-                    if k > 0:
-                        expected(k, 1)
-                    apply_gain(k, 0)
+            if live(n + 1):
+                normalise(n + 1, 0)
+            prepare_post(n, 3)
 
+        pairs_transpose("S", last - 1)
+        turned_out("S", last - 1)
+        pairs_transpose("Y", last - 4)
+        turned_out("Y", last - 4)
+        y_quantize(last - 5)
+        s_quantize(last - 1)
+        add_score(last - 2)
         y_round(last - 2)
-        turn_y(last - 3)
+        overlap_high(last, 1)
+        overlap_low(last, 1)
+        normalise(last, 1)
+        expected(last - 1, 0)
+        expected(last - 1, 1)
+        apply_gain(last - 1, 0)
+        apply_gain(last - 1, 1)
         pairs_transpose("S", last)
-        pairs_out(nc.scalar.copy, "S_k", last, t["S_t", last], 2)
-        add_score(last - 1)
-        turn_y(last - 2)
-        s_quantize(last)
-        y_round(last - 1)
+        turned_out("S", last)
+        pairs_transpose("Y", last - 3)
+        turned_out("Y", last - 3)
+        pairs_transpose("Y", last - 2)
+        turned_out("Y", last - 2)
         y_quantize(last - 4)
+        s_quantize(last)
+        add_score(last - 1)
+        y_round(last - 1)
         expected(last, 0)
         expected(last, 1)
-        y_quantize(last - 3)
-        y_quantize(last - 2)
-        turn_y(last - 1)
         apply_gain(last, 0)
         apply_gain(last, 1)
-        last_tile(last)
+        half_add(last, 0)
+        half_add(last, 1)
+        half_round(last, 0, nc.scalar.copy)
+        y_quantize(last - 3)
+        half_round(last, 1, nc.vector.tensor_copy)
+        y_quantize(last - 2)
+        pairs_transpose("Y", last - 1)
+        turned_out("Y", last - 1)
+        half_turn(last, 0, nc.scalar.copy)
+        y_quantize(last - 1)
+        half_turn(last, 1, nc.vector.tensor_copy)
+        half_quantize(last, 0)
+        half_quantize(last, 1)
 
         scale_out = out_2.rearrange("g q m -> q g m").bitcast(I32)
         for quad in range(4):

@@ -17,11 +17,13 @@ ACT = mybir.ActivationFunctionType
 ALU = mybir.AluOpType
 
 P = 128
-NT = C // P
-BANK = 512
-POOL_UNTIL = 7
-POST_PLAN = {(0,2): [((0,0),"V"),((0,1),"S")], (0,3): [((0,0),"Q")], (1,0): [((0,1),"Q")], (1,1): [((1,0),"V")], (1,2): [((1,1),"S"),((1,0),"Q")], (2,0): [((1,1),"Q")]}
+GROUP = 512
+HALF = 512
+PAIRS = GROUP // 2
+TILES = C // P
+LAST = TILES - 1
 SORT_FROM = 4
+ROUND_ON_GPSIMD = range(1, TILES - 3)
 
 
 def tile_mbr_expected_overlap_k6_kernel(
@@ -29,452 +31,431 @@ def tile_mbr_expected_overlap_k6_kernel(
     out_0, out_1, out_2,
 ):
     nc = tc.nc
+    on_vector = nc.vector.tensor_copy
+    on_scalar = nc.scalar.copy
     with ExitStack() as ctx:
         keep = ctx.enter_context(tc.tile_pool(name="keep", bufs=1))
         work = ctx.enter_context(tc.tile_pool(name="work", bufs=2))
         psum = ctx.enter_context(tc.psum_pool(name="psum", bufs=8))
         ctx.enter_context(tc.manual_schedule())
 
-        t = {}
+        tiles = {}
 
-        def sb(kind, key, shape, dtype, bufs=2):
-            t[kind, key] = work.tile(shape, dtype, name=kind, tag=kind, bufs=bufs, align_bytes=64)
-            return t[kind, key]
+        def new_tile(kind, key, shape, dtype, bufs=2):
+            tiles[kind, key] = work.tile(shape, dtype, name=kind, tag=kind, bufs=bufs, align_bytes=64)
+            return tiles[kind, key]
 
-        def const(name, shape, dtype):
+        def kept_tile(name, shape, dtype):
             return keep.tile(shape, dtype, name=name, tag=name, align_bytes=64)
 
-        def tbank(kind, key):
-            t[kind, key] = psum.tile([P, 4, P], F32, name="bank", tag="bank")
-            return t[kind, key]
+        def new_bank(kind, key, shape):
+            tiles[kind, key] = psum.tile(shape, F32, name="bank", tag="bank")
+            return tiles[kind, key]
 
-        def abank(kind, key):
-            t[kind, key] = psum.tile([P, BANK], F32, name="bank", tag="bank")
-            return t[kind, key]
+        def half_cols(h):
+            return slice(h * HALF, (h + 1) * HALF)
 
-        ident = const("ident", [P, P], F32)
-        len_pad = const("len_pad", [P, P], F32)
-        len_rows = const("len_rows", [NT, P], BF16)
-        warm = const("warm", [P, 2], F32)
-        rl_col = const("rl_col", [P, 2, 4], BF16)
-        gain_col = const("gain_col", [P, 2, 4], BF16)
-        lnrl_col = const("lnrl_col", [P, 8], F32)
-        gain_col32 = const("gain_col32", [P, 8], F32)
-        ln_cl = const("ln_cl", [P, NT], F32)
-        inv_cl = const("inv_cl", [P, NT], F32)
-        lnrl_all = const("lnrl_all", [P, R], F32)
-        gain_all = const("gain_all", [P, Q], F32)
-        rh_scales = const("rh_scales", [P, 4, R], U8)
-        rh_words = [const("rh_words%d" % h, [P, 4, 2 * BANK], U8) for h in range(2)]
-        y_scales = const("y_scales", [P, 2, C], U8)
+        ident = kept_tile("ident", [P, P], F32)
+        len_rows = kept_tile("len_rows", [TILES, P], BF16)
+        len_square = kept_tile("len_square", [P, P], F32)
+        ln_cand_len = kept_tile("ln_cand_len", [P, TILES], F32)
+        inv_cand_len = kept_tile("inv_cand_len", [P, TILES], F32)
+        ref_len_cols = kept_tile("ref_len_cols", [P, 2, 4], BF16)
+        gain_cols = kept_tile("gain_cols", [P, 2, 4], BF16)
+        ln_ref_len_cols = kept_tile("ln_ref_len_cols", [P, 8], F32)
+        gain_cols_f32 = kept_tile("gain_cols_f32", [P, 8], F32)
+        ln_ref_len = kept_tile("ln_ref_len", [P, R], F32)
+        gain_row = kept_tile("gain_row", [P, Q], F32)
+        rh_scales = kept_tile("rh_scales", [P, K2 // GROUP, R], U8)
+        rh_words = [kept_tile("rh_words%d" % h, [P, K2 // GROUP, 2 * HALF], U8) for h in range(2)]
+        y_scales = kept_tile("y_scales", [P, Q // GROUP, C], U8)
 
-        def load_cand_high(i):
-            x = sb("cand_hi", i, [P, K2], BF16, bufs=5)
-            nc.sync.dma_start(out=x[:], in_=cand_high[i * P:(i + 1) * P, :])
+        def load_cand_part(kind, i):
+            src = cand_high if kind == "hi" else cand_low
+            x = new_tile("cand_" + kind, i, [P, src.shape[1]], BF16, bufs=5)
+            nc.sync.dma_start(out=x[:], in_=src[i * P:(i + 1) * P, :])
 
-        def load_cand_low(i):
-            x = sb("cand_lo", i, [P, K1], BF16, bufs=5)
-            nc.sync.dma_start(out=x[:], in_=cand_low[i * P:(i + 1) * P, :])
+        def load_cand(i):
+            load_cand_part("hi", i)
+            load_cand_part("lo", i)
 
         def load_score(i):
-            x = sb("score", i, [P, Q], BF16, bufs=5)
+            x = new_tile("score", i, [P, Q], BF16, bufs=5)
             nc.sync.dma_start(out=x[:], in_=score[i * P:(i + 1) * P, :])
 
-        def load_ref_low(h):
-            x = sb("ref_raw", h, [P, 4, BANK], BF16)
-            nc.sync.dma_start(out=x[:], in_=ref_low.rearrange("(p j) n -> p j n", j=4)[:, :, h * BANK:(h + 1) * BANK])
-            t["rows_raw", ("ref", h)] = x[:]
+        def load_vector_cols(cols, vector):
+            nc.sync.dma_start(out=cols[:], in_=vector.rearrange("(h p t) -> p h t", h=2, t=4))
 
-        def load_post(h):
-            x = sb("post_raw", h, [P, 4, Q], BF16)
-            nc.sync.dma_start(out=x[:], in_=post[h * BANK:(h + 1) * BANK, :].rearrange("(p j) n -> p j n", j=4))
-            for half in range(2):
-                t["rows_raw", ("post", h, half)] = x[:, :, half * BANK:(half + 1) * BANK]
+        def load_ref_high(h):
+            rows = ref_high_words.rearrange("g p b -> p g b")[:, :, h * 2 * HALF:(h + 1) * 2 * HALF]
+            nc.sync.dma_start(out=rh_words[h][:].bitcast(I32), in_=rows.bitcast(I32))
+
+        def load_ref_low(h):
+            x = new_tile("ref_raw", h, [P, 4, HALF], BF16)
+            nc.sync.dma_start(out=x[:], in_=ref_low.rearrange("(p t) n -> p t n", t=4)[:, :, half_cols(h)])
+            tiles["rows_raw", ("ref", h)] = x[:]
+
+        def load_post(g):
+            x = new_tile("post_raw", g, [P, 4, Q], BF16)
+            nc.sync.dma_start(out=x[:], in_=post[g * GROUP:(g + 1) * GROUP, :].rearrange("(p t) n -> p t n", t=4))
+            for h in range(2):
+                tiles["rows_raw", ("post", g, h)] = x[:, :, half_cols(h)]
 
         def interleave_rows(key, copy):
-            x = sb("rows_il", key, [P, 4 * BANK], BF16, bufs=3)
+            x = new_tile("rows_k", key, [P, 4 * HALF], BF16, bufs=3)
             copy(
-                out=x[:].rearrange("p (c i j) -> p c j i", i=4, j=4),
-                in_=t["rows_raw", key].rearrange("p j (c i) -> p c j i", i=4),
+                out=x[:].rearrange("p (c i t) -> p c t i", i=4, t=4),
+                in_=tiles["rows_raw", key].rearrange("p t (c i) -> p c t i", i=4),
             )
 
         def quantize_rows(key):
-            codes = sb("rows_codes", key, [P, BANK], U32, bufs=6)
-            scales = sb("rows_scales", key, [P, BANK], U8, bufs=6)
-            nc.vector.quantize_mx(out=codes[:].bitcast(FP8X4), scales=scales[:], in_=t["rows_il", key][:])
+            codes = new_tile("rows_codes", key, [P, HALF], U32, bufs=6)
+            scales = new_tile("rows_scales", key, [P, HALF], U8, bufs=6)
+            nc.vector.quantize_mx(out=codes[:].bitcast(FP8X4), scales=scales[:], in_=tiles["rows_k", key][:])
+
+        def spread(name, cols):
+            for h in range(2):
+                bank = new_bank(name, h, [P, HALF])
+                for t in range(4):
+                    j = 4 * h + t
+                    nc.tensor.transpose(bank[:, t * P:(t + 1) * P], cols[:, j:j + 1].to_broadcast([P, P]), ident[:])
+
+        def pairs_out(copy, x, bank, groups):
+            copy(out=x, in_=bank[:, 0:2 * groups, :].rearrange("p (g u) c -> p g c u", u=2))
+
+        def as_pairs(x, groups):
+            return x.bitcast(F32).rearrange("p (g c u) -> p g c u", g=groups, u=2)
+
+        def turn_groups(kind, i, groups):
+            words = tiles[kind, i][:].bitcast(F32)
+            bank = new_bank(kind + "_turned", (i, groups[0]), [P, 4, P])
+            for n, g in enumerate(groups):
+                for u in range(2):
+                    first = g * PAIRS + u * P
+                    nc.tensor.transpose(bank[:, 2 * n + u, :], words[:, first:first + P], ident[:])
+            return bank
 
         def cand_sort(i, kind, copy):
             groups = 4 if kind == "hi" else 1
-            x = sb("cand_sorted_" + kind, i, [P, groups * 256], F32)
+            x = new_tile("cand_sorted_" + kind, i, [P, groups * PAIRS], F32)
             copy(
                 out=x[:].rearrange("c (g u p) -> c g u p", g=groups, u=2),
-                in_=t["cand_" + kind, i][:].bitcast(F32).rearrange("c (g p u) -> c g u p", g=groups, u=2),
+                in_=tiles["cand_" + kind, i][:].bitcast(F32).rearrange("c (g p u) -> c g u p", g=groups, u=2),
             )
 
-        def cand_transpose(i, part):
-            groups = 2 if part < 2 else 1
-            kind = "hi" if part < 2 else "lo"
-            first = 512 * part if part < 2 else 0
-            bank = tbank("cand_t", (i, part))
-            for g in range(groups):
-                for u in range(2):
-                    lo = first + 256 * g
-                    if i >= SORT_FROM:
-                        src = t["cand_sorted_" + kind, i][:, lo + P * u:lo + P * (u + 1)]
-                    else:
-                        src = t["cand_" + kind, i][:].bitcast(F32)[:, lo + u:lo + 256:2]
-                    nc.tensor.transpose(bank[:, 2 * g + u, :], src, ident[:])
+        def cand_turn(i):
+            for kind, first_group, groups in (("hi", 0, 2), ("hi", 2, 2), ("lo", 0, 1)):
+                bank = new_bank("cand_turned", (i, kind, first_group), [P, 4, P])
+                for g in range(groups):
+                    for u in range(2):
+                        first = (first_group + g) * PAIRS
+                        if i >= SORT_FROM:
+                            src = tiles["cand_sorted_" + kind, i][:, first + P * u:first + P * (u + 1)]
+                        else:
+                            src = tiles["cand_" + kind, i][:].bitcast(F32)[:, first + u:first + PAIRS:2]
+                        nc.tensor.transpose(bank[:, 2 * g + u, :], src, ident[:])
+                if first_group == 0:
+                    new_tile("cand_k_" + kind, i, [P, K2 if kind == "hi" else K1], BF16)
+                x = tiles["cand_k_" + kind, i][:, first_group * GROUP:(first_group + groups) * GROUP]
+                pairs_out(on_scalar, as_pairs(x, groups), bank, groups)
 
-        def pairs_out(copy, x, bank, groups):
-            copy(
-                out=x.bitcast(F32).rearrange("p (g c u) -> p g c u", g=groups, u=2),
-                in_=bank[:, 0:2 * groups, :].rearrange("p (g u) c -> p g c u", u=2),
-            )
-
-        def cand_copy(i, part, copy=nc.scalar.copy):
-            if part == 0:
-                sb("cand_k_hi", i, [P, K2], BF16)
-            if part == 2:
-                sb("cand_k_lo", i, [P, K1], BF16)
-                pairs_out(nc.scalar.copy, t["cand_k_lo", i][:], t["cand_t", (i, part)], 1)
-            else:
-                pairs_out(copy, t["cand_k_hi", i][:, 1024 * part:1024 * (part + 1)], t["cand_t", (i, part)], 2)
-
-        def cand_quantize(i, kind, parts=1):
+        def cand_quantize(i, kind):
             width = 4 * P if kind == "hi" else P
-            codes = sb("cand_codes_" + kind, i, [P, width], U32)
-            scales = sb("cand_scales_" + kind, i, [P, width], U8)
-            step = width // parts
-            for lo in range(0, width, step):
+            step = 2 * P if kind == "hi" else P
+            codes = new_tile("cand_codes_" + kind, i, [P, width], U32)
+            scales = new_tile("cand_scales_" + kind, i, [P, width], U8)
+            for first in range(0, width, step):
                 nc.vector.quantize_mx(
-                    out=codes[:, lo:lo + step].bitcast(FP8X4), scales=scales[:, lo:lo + step],
-                    in_=t["cand_k_" + kind, i][:, 4 * lo:4 * (lo + step)],
+                    out=codes[:, first:first + step].bitcast(FP8X4), scales=scales[:, first:first + step],
+                    in_=tiles["cand_k_" + kind, i][:, 4 * first:4 * (first + step)],
                 )
 
-        def overlap_high(i, h):
-            acc = abank("O", (i, h))
-            for g in range(4):
-                cols = slice(g * P, (g + 1) * P)
+        def overlap(i, h):
+            acc = new_bank("O", (i, h), [P, HALF])
+            for g in range(K2 // GROUP):
+                rows = slice(g * P, (g + 1) * P)
                 nc.tensor.matmul_mx(
                     out=acc[:],
-                    lhsT=t["cand_codes_hi", i][:, cols].bitcast(FP8X4),
-                    lhsT_scale=t["cand_scales_hi", i][:, cols],
+                    lhsT=tiles["cand_codes_hi", i][:, rows].bitcast(FP8X4),
+                    lhsT_scale=tiles["cand_scales_hi", i][:, rows],
                     rhs=rh_words[h][:, g, :].bitcast(FP4X4),
-                    rhs_scale=rh_scales[:, g, h * BANK:(h + 1) * BANK],
+                    rhs_scale=rh_scales[:, g, half_cols(h)],
                     start=(g == 0), stop=False,
                 )
-
-        def overlap_low(i, h):
             nc.tensor.matmul_mx(
-                out=t["O", (i, h)][:],
-                lhsT=t["cand_codes_lo", i][:].bitcast(FP8X4),
-                lhsT_scale=t["cand_scales_lo", i][:],
-                rhs=t["rows_codes", ("ref", h)][:].bitcast(FP8X4),
-                rhs_scale=t["rows_scales", ("ref", h)][:],
+                out=acc[:],
+                lhsT=tiles["cand_codes_lo", i][:].bitcast(FP8X4),
+                lhsT_scale=tiles["cand_scales_lo", i][:],
+                rhs=tiles["rows_codes", ("ref", h)][:].bitcast(FP8X4),
+                rhs_scale=tiles["rows_scales", ("ref", h)][:],
                 start=False, stop=True,
             )
 
-        def share(i):
-            x = sb("share", i, [P, R], F32)
-            nc.scalar.activation(out=x[:], in_=lnrl_all[:], func=ACT.Sigmoid, bias=ln_cl[:, i:i + 1], scale=-1.0)
+        def length_share(i):
+            x = new_tile("share", i, [P, R], F32)
+            nc.scalar.activation(
+                out=x[:], in_=ln_ref_len[:], func=ACT.Sigmoid, bias=ln_cand_len[:, i:i + 1], scale=-1.0,
+            )
 
         def normalise(i, h):
             if h == 0:
-                sb("S", i, [P, R], BF16)
+                new_tile("S", i, [P, R], BF16)
             for u in range(2):
-                cols = slice(h * BANK + u * 256, h * BANK + (u + 1) * 256)
+                cols = slice(h * HALF + u * 2 * P, h * HALF + (u + 1) * 2 * P)
                 nc.vector.scalar_tensor_tensor(
-                    out=t["S", i][:, cols].rearrange("c (p e) -> c p e", e=2),
-                    in0=t["O", (i, h)][:].rearrange("c (p u e) -> c u p e", u=2, e=2)[:, u, :, :],
-                    scalar=inv_cl[:, i:i + 1],
-                    in1=t["share", i][:, cols].rearrange("c (p e) -> c p e", e=2),
+                    out=tiles["S", i][:, cols].rearrange("c (p e) -> c p e", e=2),
+                    in0=tiles["O", (i, h)][:].rearrange("c (p u e) -> c u p e", u=2, e=2)[:, u, :, :],
+                    scalar=inv_cand_len[:, i:i + 1],
+                    in1=tiles["share", i][:, cols].rearrange("c (p e) -> c p e", e=2),
                     op0=ALU.mult, op1=ALU.mult,
                 )
 
-        def pairs_transpose(kind, i):
-            words = t[kind, i][:].bitcast(F32)
-            bank = tbank(kind + "_t", i)
-            for j in range(4):
-                nc.tensor.transpose(bank[:, j, :], words[:, j * P:(j + 1) * P], ident[:])
+        def s_turn(i, groups=(0, 1)):
+            bank = turn_groups("S", i, groups)
+            if groups[0] == 0:
+                new_tile("S_k", i, [P, R], BF16, bufs=3)
+            x = tiles["S_k", i][:, groups[0] * GROUP:(groups[-1] + 1) * GROUP]
+            pairs_out(on_scalar, as_pairs(x, len(groups)), bank, len(groups))
 
-        def s_quantize(i):
-            codes = sb("S_codes", i, [P, 2 * P], U32, bufs=4)
-            scales = sb("S_scales", i, [P, 2 * P], U8, bufs=4)
-            nc.vector.quantize_mx(out=codes[:].bitcast(FP8X4), scales=scales[:], in_=t["S_k", i][:])
+        def s_quantize(i, groups=(0, 1)):
+            if groups[0] == 0:
+                new_tile("S_codes", i, [P, 2 * P], U32, bufs=4)
+                new_tile("S_scales", i, [P, 2 * P], U8, bufs=4)
+            rows = slice(groups[0] * P, (groups[-1] + 1) * P)
+            nc.vector.quantize_mx(
+                out=tiles["S_codes", i][:, rows].bitcast(FP8X4), scales=tiles["S_scales", i][:, rows],
+                in_=tiles["S_k", i][:, groups[0] * GROUP:(groups[-1] + 1) * GROUP],
+            )
 
-        def expected(i, half):
-            acc = abank("U", (i, half))
-            for h in range(2):
+        def expected(i, h, groups=(0, 1)):
+            if groups[0] == 0:
+                new_bank("U", (i, h), [P, HALF])
+            for g in groups:
+                rows = slice(g * P, (g + 1) * P)
                 nc.tensor.matmul_mx(
-                    out=acc[:],
-                    lhsT=t["S_codes", i][:, h * P:(h + 1) * P].bitcast(FP8X4),
-                    lhsT_scale=t["S_scales", i][:, h * P:(h + 1) * P],
-                    rhs=t["rows_codes", ("post", h, half)][:].bitcast(FP8X4),
-                    rhs_scale=t["rows_scales", ("post", h, half)][:],
-                    start=(h == 0), stop=(h == 1),
+                    out=tiles["U", (i, h)][:],
+                    lhsT=tiles["S_codes", i][:, rows].bitcast(FP8X4),
+                    lhsT_scale=tiles["S_scales", i][:, rows],
+                    rhs=tiles["rows_codes", ("post", g, h)][:].bitcast(FP8X4),
+                    rhs_scale=tiles["rows_scales", ("post", g, h)][:],
+                    start=(g == 0), stop=(g == 1),
                 )
 
-        def apply_gain(i, half):
-            if half == 0:
-                sb("scaled", i, [P, Q], F32, bufs=3)
-            cols = slice(half * BANK, (half + 1) * BANK)
-            nc.vector.tensor_tensor(out=t["scaled", i][:, cols], in0=t["U", (i, half)][:], in1=gain_all[:, cols], op=ALU.mult)
+        def apply_gain(i, h):
+            if h == 0:
+                new_tile("scaled", i, [P, Q], F32, bufs=3)
+            nc.vector.tensor_tensor(
+                out=tiles["scaled", i][:, half_cols(h)], in0=tiles["U", (i, h)][:], in1=gain_row[:, half_cols(h)],
+                op=ALU.mult,
+            )
 
-        def add_score(i):
-            y = sb("y", i, [P, Q], F32, bufs=4)
-            nc.vector.tensor_tensor(out=y[:], in0=t["scaled", i][:], in1=t["score", i][:], op=ALU.add)
-            nc.sync.dma_start(out=out_0[i * P:(i + 1) * P, :], in_=y[:])
+        def second_stage(i):
+            for h in range(2):
+                expected(i, h)
+            for h in range(2):
+                apply_gain(i, h)
+
+        def add_score(i, cols=slice(0, Q)):
+            if cols.start == 0:
+                new_tile("y", i, [P, Q], F32, bufs=4)
+            y = tiles["y", i][:, cols]
+            nc.vector.tensor_tensor(out=y, in0=tiles["scaled", i][:, cols], in1=tiles["score", i][:, cols], op=ALU.add)
+            nc.sync.dma_start(out=out_0[i * P:(i + 1) * P, cols], in_=y)
+
+        def y_round_group(i, g, copy):
+            if g == 0:
+                new_tile("Y", i, [P, Q], BF16, bufs=3)
+            copy(
+                out=tiles["Y", i][:, half_cols(g)].rearrange("c (u p e) -> c u p e", u=2, e=2),
+                in_=tiles["y", i][:, half_cols(g)].rearrange("c (p u e) -> c u p e", u=2, e=2),
+            )
+
+        def on_gpsimd(out, in_):
+            nc.gpsimd.tensor_scalar(out=out, in0=in_, scalar1=1.0, scalar2=0.0, op0=ALU.mult, op1=ALU.add)
 
         def y_round(i):
-            x = sb("Y", i, [P, Q], BF16, bufs=3)
-            if 0 < i < POOL_UNTIL:
+            if i in ROUND_ON_GPSIMD:
                 for g in range(2):
-                    cols = slice(g * BANK, (g + 1) * BANK)
-                    nc.gpsimd.tensor_scalar(
-                        out=x[:, cols].rearrange("c (u p e) -> c u p e", u=2, e=2),
-                        in0=t["y", i][:, cols].rearrange("c (p u e) -> c u p e", u=2, e=2),
-                        scalar1=1.0, scalar2=0.0, op0=ALU.mult, op1=ALU.add,
-                    )
+                    y_round_group(i, g, on_gpsimd)
             else:
-                nc.scalar.copy(
+                x = new_tile("Y", i, [P, Q], BF16, bufs=3)
+                on_scalar(
                     out=x[:].rearrange("c (g u p e) -> c g u p e", g=2, u=2, e=2),
-                    in_=t["y", i][:].rearrange("c (g p u e) -> c g u p e", g=2, u=2, e=2),
+                    in_=tiles["y", i][:].rearrange("c (g p u e) -> c g u p e", g=2, u=2, e=2),
                 )
 
-        def turned_out(kind, i):
-            x = sb(kind + "_k", i, [P, 2 * 4 * P], BF16, bufs=3)
-            pairs_out(nc.scalar.copy, x[:], t[kind + "_t", i], 2)
+        def y_turn(i, groups=(0, 1), copy=on_scalar):
+            bank = turn_groups("Y", i, groups)
+            if i % 2 == 0:
+                new_tile("Y_k", i // 2, [P, 2, 2 * 4 * P], BF16, bufs=3)
+            x = tiles["Y_k", i // 2][:, groups[0]:groups[-1] + 1, (i % 2) * 4 * P:(i % 2 + 1) * 4 * P]
+            pairs_out(copy, x.bitcast(F32).rearrange("p g (c u) -> p g c u", u=2), bank, len(groups))
 
         words_out = out_1.rearrange("g p m t -> p g (m t)").bitcast(I32)
+        scales_out = out_2.rearrange("g q m -> q g m").bitcast(I32)
 
-        def y_quantize(i):
-            if i % 2 == 0:
-                sb("y_codes", i // 2, [P, 2, 2 * P], U32, bufs=3)
-            codes = t["y_codes", i // 2]
-            for g in range(2):
-                nc.vector.quantize_mx(
-                    out=codes[:, g, (i % 2) * P:(i % 2 + 1) * P].bitcast(FP8X4),
-                    scales=y_scales[:, g, i * P:(i + 1) * P],
-                    in_=t["Y_k", i][:, g * BANK:(g + 1) * BANK],
-                )
-            if i % 2 == 1:
-                nc.sync.dma_start(out=words_out[:, :, (i - 1) * P:(i + 1) * P], in_=codes[:].bitcast(I32))
-
-        def half_add(i, g):
+        def y_quantize(couple, g):
             if g == 0:
-                sb("y", i, [P, Q], F32, bufs=4)
-            cols = slice(g * BANK, (g + 1) * BANK)
-            nc.vector.tensor_tensor(out=t["y", i][:, cols], in0=t["scaled", i][:, cols], in1=t["score", i][:, cols], op=ALU.add)
-            nc.sync.dma_start(out=out_0[i * P:(i + 1) * P, cols], in_=t["y", i][:, cols])
-
-        def half_round(i, g, copy):
-            if g == 0:
-                sb("Y", i, [P, Q], BF16, bufs=3)
-            cols = slice(g * BANK, (g + 1) * BANK)
-            copy(
-                out=t["Y", i][:, cols].rearrange("c (u p e) -> c u p e", u=2, e=2),
-                in_=t["y", i][:, cols].rearrange("c (p u e) -> c u p e", u=2, e=2),
-            )
-
-        def half_turn(i, g, copy):
-            if g == 0:
-                sb("Y_k", i, [P, 2 * 4 * P], BF16, bufs=3)
-            bank = tbank("Y_t", (i, g))
-            for u in range(2):
-                lo = (2 * g + u) * P
-                nc.tensor.transpose(bank[:, u, :], t["Y", i][:].bitcast(F32)[:, lo:lo + P], ident[:])
-            pairs_out(copy, t["Y_k", i][:, g * BANK:(g + 1) * BANK], bank, 1)
-
-        def half_quantize(i, g):
-            codes = t["y_codes", i // 2]
+                new_tile("y_codes", couple, [P, 2, 2 * P], U32, bufs=3)
+            rows = slice(couple * 2 * P, (couple + 1) * 2 * P)
+            codes = tiles["y_codes", couple]
             nc.vector.quantize_mx(
-                out=codes[:, g, P:2 * P].bitcast(FP8X4),
-                scales=y_scales[:, g, i * P:(i + 1) * P],
-                in_=t["Y_k", i][:, g * BANK:(g + 1) * BANK],
+                out=codes[:, g, :].bitcast(FP8X4), scales=y_scales[:, g, rows], in_=tiles["Y_k", couple][:, g, :],
             )
-            nc.sync.dma_start(out=words_out[:, g, (i - 1) * P:(i + 1) * P], in_=codes[:, g, :].bitcast(I32))
-
-        def spread(col, name):
-            for h in range(2):
-                bank = abank(name, h)
-                for j in range(4):
-                    nc.tensor.transpose(bank[:, j * P:(j + 1) * P], col[:, 4 * h + j:4 * h + j + 1].to_broadcast([P, P]), ident[:])
+            if couple == LAST // 2:
+                nc.sync.dma_start(out=words_out[:, g, rows], in_=codes[:, g, :].bitcast(I32))
+            elif g == 1:
+                nc.sync.dma_start(out=words_out[:, :, rows], in_=codes[:].bitcast(I32))
 
         nc.vector.memset(rh_scales[:].rearrange("p g n -> p (g n)").bitcast(I32), 0)
-        nc.vector.memset(len_pad[:], 1.0)
+        nc.vector.memset(len_square[:], 1.0)
         make_identity(nc, ident[:])
-        nc.scalar.activation(out=warm[:, 0:1], in_=len_pad[:, P - 1:P], func=ACT.Ln)
 
-        def load_ref_high(h):
-            nc.sync.dma_start(out=rh_words[h][:].bitcast(I32), in_=word_rows[:, :, h * 2 * BANK:(h + 1) * 2 * BANK].bitcast(I32))
-
-        scale_rows = ref_high_scales.rearrange("g q n -> q g n").bitcast(I32)
-        word_rows = ref_high_words.rearrange("g p b -> p g b")
-        nc.sync.dma_start(out=rl_col[:], in_=ref_len.rearrange("(h p j) -> p h j", h=2, j=4))
+        load_cand_part("hi", 0)
+        load_vector_cols(ref_len_cols, ref_len)
         nc.sync.dma_start(out=len_rows[:], in_=cand_len.rearrange("(i p) -> i p", p=P))
-        nc.sync.dma_start(out=gain_col[:], in_=gain.rearrange("(h p j) -> p h j", h=2, j=4))
+        load_cand_part("lo", 0)
         load_ref_low(0)
-        load_cand_high(0)
-        load_cand_low(0)
         load_ref_high(0)
+        scale_rows = ref_high_scales.rearrange("g q n -> q g n").bitcast(I32)
         for quad in range(4):
-            nc.sync.dma_start(out=rh_scales[32 * quad:32 * quad + 4, :, :].bitcast(I32), in_=scale_rows[4 * quad:4 * quad + 4, :, :])
-        load_cand_high(1)
-        load_cand_low(1)
+            nc.sync.dma_start(
+                out=rh_scales[32 * quad:32 * quad + 4, :, :].bitcast(I32), in_=scale_rows[4 * quad:4 * quad + 4, :, :],
+            )
+        load_vector_cols(gain_cols, gain)
         load_ref_low(1)
+        load_cand(1)
         load_ref_high(1)
         load_post(0)
-        load_cand_high(2)
-        load_cand_low(2)
+        load_cand(2)
         load_post(1)
-        load_cand_high(3)
-        load_cand_low(3)
+        load_cand(3)
 
-        nc.scalar.activation(out=lnrl_col[:], in_=rl_col[:].rearrange("p h j -> p (h j)"), func=ACT.Ln)
-        nc.vector.tensor_copy(out=len_pad[0:NT, :], in_=len_rows[:])
-        nc.vector.tensor_copy(out=gain_col32[:], in_=gain_col[:].rearrange("p h j -> p (h j)"))
-        len_t = tbank("len_t", 0)
-        nc.tensor.transpose(len_t[:, 0, :], len_pad[:], ident[:])
-        spread(lnrl_col, "lnrl_t")
-        spread(gain_col32, "gain_t")
-        nc.scalar.activation(out=ln_cl[:], in_=len_t[:, 0, 0:NT], func=ACT.Ln)
-        nc.vector.reciprocal(out=inv_cl[:], in_=len_t[:, 0, 0:NT])
-        nc.scalar.activation(out=warm[:, 1:2], in_=ln_cl[:, 0:1], func=ACT.Sigmoid)
-        for h in range(2):
-            nc.scalar.copy(
-                out=lnrl_all[:, h * BANK:(h + 1) * BANK].rearrange("c (u p e) -> c u p e", u=2, e=2),
-                in_=t["lnrl_t", h][:].rearrange("c (u e p) -> c u p e", u=2, e=2),
-            )
-        interleave_rows(("ref", 0), nc.vector.tensor_copy)
+        nc.scalar.activation(out=ln_ref_len_cols[:], in_=ref_len_cols[:].rearrange("p h t -> p (h t)"), func=ACT.Ln)
+        on_vector(out=len_square[0:TILES, :], in_=len_rows[:])
+        cand_turn(0)
+        len_turned = new_bank("len_turned", 0, [P, 4, P])
+        nc.tensor.transpose(len_turned[:, 0, :], len_square[:], ident[:])
+        spread("ln_ref_len_turned", ln_ref_len_cols)
+        nc.scalar.activation(out=ln_cand_len[:], in_=len_turned[:, 0, 0:TILES], func=ACT.Ln)
+        interleave_rows(("ref", 0), on_vector)
+        cand_quantize(0, "hi")
         quantize_rows(("ref", 0))
-        for part in range(3):
-            cand_transpose(0, part)
-            cand_copy(0, part, nc.vector.tensor_copy if part == 0 else nc.scalar.copy)
-        cand_quantize(0, "hi", parts=2)
         cand_quantize(0, "lo")
-        share(0)
-        overlap_high(0, 0)
-        overlap_low(0, 0)
-        interleave_rows(("ref", 1), nc.vector.tensor_copy)
+        nc.vector.reciprocal(out=inv_cand_len[:], in_=len_turned[:, 0, 0:TILES])
         for h in range(2):
-            nc.scalar.copy(
-                out=gain_all[:, h * BANK:(h + 1) * BANK].rearrange("c (p j) -> c p j", j=4),
-                in_=t["gain_t", h][:].rearrange("c (j p) -> c p j", j=4),
+            on_scalar(
+                out=ln_ref_len[:, half_cols(h)].rearrange("c (u p e) -> c u p e", u=2, e=2),
+                in_=tiles["ln_ref_len_turned", h][:].rearrange("c (u e p) -> c u p e", u=2, e=2),
             )
+        length_share(0)
+        on_vector(out=gain_cols_f32[:], in_=gain_cols[:].rearrange("p h t -> p (h t)"))
+        overlap(0, 0)
+        spread("gain_turned", gain_cols_f32)
+        for h in range(2):
+            on_scalar(
+                out=gain_row[:, half_cols(h)].rearrange("c (p t) -> c p t", t=4),
+                in_=tiles["gain_turned", h][:].rearrange("c (t p) -> c p t", t=4),
+            )
+        interleave_rows(("ref", 1), on_vector)
         normalise(0, 0)
         quantize_rows(("ref", 1))
 
-        def live(i):
-            return 0 <= i < NT
-
-        def prepare_post(n, slot):
-            for key, step in POST_PLAN.get((n, slot), []):
-                if step == "Q":
-                    quantize_rows(("post",) + key)
-                else:
-                    interleave_rows(("post",) + key, nc.vector.tensor_copy if step == "V" else nc.scalar.copy)
-
-        last = NT - 1
-        for n in range(last):
-            if live(n - 1):
+        for n in range(LAST):
+            if n >= 1:
                 load_score(n - 1)
-            if n == last - 1:
-                load_score(last - 1)
-                load_score(last)
-            if live(n + 4):
-                load_cand_high(n + 4)
-                load_cand_low(n + 4)
-            if live(n - 1):
-                pairs_transpose("S", n - 1)
-                turned_out("S", n - 1)
-            if live(n + 1):
-                for part in range(3):
-                    cand_transpose(n + 1, part)
-                    cand_copy(n + 1, part)
-            for k in ([n - 4] if n >= 4 else []):
-                pairs_transpose("Y", k)
-                turned_out("Y", k)
-            prepare_post(n, 0)
-            if live(n - 1):
+            if n == LAST - 1:
+                load_score(LAST - 1)
+                load_score(LAST)
+            if n + 4 <= LAST:
+                load_cand(n + 4)
+
+            if n >= 1:
+                s_turn(n - 1)
+            cand_turn(n + 1)
+            if n >= 4:
+                y_turn(n - 4)
+            if n == 1:
+                quantize_rows(("post", 0, 1))
+            if n == 2:
+                quantize_rows(("post", 1, 1))
+            if n >= 1:
                 s_quantize(n - 1)
-            for k in ([n - 5] if n >= 5 else []):
-                y_quantize(k)
-            if live(n + 2) and n + 2 >= SORT_FROM:
-                cand_sort(n + 2, "lo", nc.vector.tensor_copy)
-            if live(n + 1):
-                cand_quantize(n + 1, "hi", parts=2)
-                cand_quantize(n + 1, "lo")
-            prepare_post(n, 1)
-            if live(n + 1):
-                share(n + 1)
-            if live(n + 2) and n + 2 >= SORT_FROM:
-                cand_sort(n + 2, "hi", nc.scalar.copy)
+            if n >= 6:
+                y_quantize((n - 6) // 2, n % 2)
+            sort_ahead = SORT_FROM <= n + 2 <= LAST
+            if sort_ahead:
+                cand_sort(n + 2, "lo", on_vector)
+            cand_quantize(n + 1, "hi")
+            cand_quantize(n + 1, "lo")
+            length_share(n + 1)
+            if sort_ahead:
+                cand_sort(n + 2, "hi", on_scalar)
             if n == 3:
                 y_round(0)
             if n >= 3:
                 add_score(n - 2)
                 y_round(n - 2)
-            overlap_high(n, 1)
-            overlap_low(n, 1)
+
+            overlap(n, 1)
             normalise(n, 1)
-            prepare_post(n, 2)
-            for k in ([] if n < 2 else [0, 1] if n == 2 else [n - 1]):
-                expected(k, 0)
-                expected(k, 1)
-                apply_gain(k, 0)
-                apply_gain(k, 1)
-            if live(n + 1):
-                overlap_high(n + 1, 0)
-                overlap_low(n + 1, 0)
+            if n == 0:
+                interleave_rows(("post", 0, 0), on_vector)
+                interleave_rows(("post", 0, 1), on_scalar)
+            if n == 1:
+                interleave_rows(("post", 1, 1), on_scalar)
+                interleave_rows(("post", 1, 0), on_vector)
+            if n == 2:
+                second_stage(0)
+            if n >= 2:
+                second_stage(n - 1)
+            overlap(n + 1, 0)
             if n == 2:
                 add_score(0)
-            if live(n + 1):
-                normalise(n + 1, 0)
-            prepare_post(n, 3)
+            normalise(n + 1, 0)
+            if n <= 1:
+                quantize_rows(("post", n, 0))
 
-        pairs_transpose("S", last - 1)
-        turned_out("S", last - 1)
-        pairs_transpose("Y", last - 4)
-        turned_out("Y", last - 4)
-        y_quantize(last - 5)
-        s_quantize(last - 1)
-        add_score(last - 2)
-        y_round(last - 2)
-        overlap_high(last, 1)
-        overlap_low(last, 1)
-        normalise(last, 1)
-        expected(last - 1, 0)
-        expected(last - 1, 1)
-        apply_gain(last - 1, 0)
-        apply_gain(last - 1, 1)
-        pairs_transpose("S", last)
-        turned_out("S", last)
-        pairs_transpose("Y", last - 3)
-        turned_out("Y", last - 3)
-        pairs_transpose("Y", last - 2)
-        turned_out("Y", last - 2)
-        y_quantize(last - 4)
-        s_quantize(last)
-        add_score(last - 1)
-        y_round(last - 1)
-        expected(last, 0)
-        expected(last, 1)
-        apply_gain(last, 0)
-        apply_gain(last, 1)
-        half_add(last, 0)
-        half_add(last, 1)
-        half_round(last, 0, nc.scalar.copy)
-        y_quantize(last - 3)
-        half_round(last, 1, nc.vector.tensor_copy)
-        y_quantize(last - 2)
-        pairs_transpose("Y", last - 1)
-        turned_out("Y", last - 1)
-        half_turn(last, 0, nc.scalar.copy)
-        y_quantize(last - 1)
-        half_turn(last, 1, nc.vector.tensor_copy)
-        half_quantize(last, 0)
-        half_quantize(last, 1)
-
-        scale_out = out_2.rearrange("g q m -> q g m").bitcast(I32)
+        s_turn(LAST - 1)
+        y_turn(LAST - 4)
+        y_quantize(1, 1)
+        s_quantize(LAST - 1)
+        add_score(LAST - 2)
+        overlap(LAST, 1)
+        s_turn(LAST, (0,))
+        y_round(LAST - 2)
+        normalise(LAST, 1)
+        for h in range(2):
+            expected(LAST - 1, h)
+        s_quantize(LAST, (0,))
+        for h in range(2):
+            apply_gain(LAST - 1, h)
+        s_turn(LAST, (1,))
+        y_turn(LAST - 3)
+        for h in range(2):
+            expected(LAST, h, (0,))
+        y_turn(LAST - 2)
+        s_quantize(LAST, (1,))
+        add_score(LAST - 1)
+        y_round(LAST - 1)
+        for h in range(2):
+            expected(LAST, h, (1,))
+        for h in range(2):
+            apply_gain(LAST, h)
+        for h in range(2):
+            add_score(LAST, half_cols(h))
+        y_round_group(LAST, 0, on_scalar)
+        y_quantize(2, 0)
+        y_round_group(LAST, 1, on_vector)
+        y_quantize(2, 1)
+        y_quantize(3, 0)
+        y_turn(LAST - 1)
+        y_turn(LAST, (0,), on_scalar)
+        y_quantize(3, 1)
+        y_turn(LAST, (1,), on_vector)
+        y_quantize(4, 0)
+        y_quantize(4, 1)
         for quad in range(4):
-            nc.sync.dma_start(out=scale_out[4 * quad:4 * quad + 4, :, :], in_=y_scales[32 * quad:32 * quad + 4, :, :].bitcast(I32))
+            nc.sync.dma_start(
+                out=scales_out[4 * quad:4 * quad + 4, :, :], in_=y_scales[32 * quad:32 * quad + 4, :, :].bitcast(I32),
+            )

from contextlib import ExitStack

import concourse.mybir as mybir
from concourse.masks import make_identity

C, R, K1, K2, Q = 1280, 1024, 512, 2048, 1024
FLOPS = 2 * C * R * (K1 + K2) + 2 * C * R * Q

F32 = mybir.dt.float32
BF16 = mybir.dt.bfloat16
I32 = mybir.dt.int32
U32 = mybir.dt.uint32
U8 = mybir.dt.uint8
FP8X4 = mybir.dt.float8_e4m3fn_x4
FP4X4 = mybir.dt.float4_e2m1fn_x4
ACT = mybir.ActivationFunctionType
ALU = mybir.AluOpType

P = 128
GROUP = 512
HALF = 512
PAIRS = GROUP // 2
TILES = C // P
LAST = TILES - 1
SORT_FROM = 4
ROUND_ON_GPSIMD = range(1, TILES - 3)


def tile_mbr_expected_overlap_k6_kernel(
    tc, cand_low, cand_high, ref_low, ref_high_words, ref_high_scales, cand_len, ref_len, post, gain, score,
    out_0, out_1, out_2,
):
    nc = tc.nc
    on_vector = nc.vector.tensor_copy
    on_scalar = nc.scalar.copy
    with ExitStack() as ctx:
        keep = ctx.enter_context(tc.tile_pool(name="keep", bufs=1))
        work = ctx.enter_context(tc.tile_pool(name="work", bufs=2))
        psum = ctx.enter_context(tc.psum_pool(name="psum", bufs=8))
        ctx.enter_context(tc.manual_schedule())

        tiles = {}

        def new_tile(kind, key, shape, dtype, bufs=2):
            tiles[kind, key] = work.tile(shape, dtype, name=kind, tag=kind, bufs=bufs, align_bytes=64)
            return tiles[kind, key]

        def kept_tile(name, shape, dtype):
            return keep.tile(shape, dtype, name=name, tag=name, align_bytes=64)

        def new_bank(kind, key, shape):
            tiles[kind, key] = psum.tile(shape, F32, name="bank", tag="bank")
            return tiles[kind, key]

        def half_cols(h):
            return slice(h * HALF, (h + 1) * HALF)

        ident = kept_tile("ident", [P, P], F32)
        len_rows = kept_tile("len_rows", [TILES, P], BF16)
        len_square = kept_tile("len_square", [P, P], F32)
        ln_cand_len = kept_tile("ln_cand_len", [P, TILES], F32)
        inv_cand_len = kept_tile("inv_cand_len", [P, TILES], F32)
        ref_len_cols = kept_tile("ref_len_cols", [P, 2, 4], BF16)
        gain_cols = kept_tile("gain_cols", [P, 2, 4], BF16)
        ln_ref_len_cols = kept_tile("ln_ref_len_cols", [P, 8], F32)
        gain_cols_f32 = kept_tile("gain_cols_f32", [P, 8], F32)
        ln_ref_len = kept_tile("ln_ref_len", [P, R], F32)
        gain_row = kept_tile("gain_row", [P, Q], F32)
        rh_scales = kept_tile("rh_scales", [P, K2 // GROUP, R], U8)
        rh_words = [kept_tile("rh_words%d" % h, [P, K2 // GROUP, 2 * HALF], U8) for h in range(2)]
        y_scales = kept_tile("y_scales", [P, Q // GROUP, C], U8)

        def load_cand_part(kind, i):
            src = cand_high if kind == "hi" else cand_low
            x = new_tile("cand_" + kind, i, [P, src.shape[1]], BF16, bufs=5)
            nc.sync.dma_start(out=x[:], in_=src[i * P:(i + 1) * P, :])

        def load_cand(i):
            load_cand_part("hi", i)
            load_cand_part("lo", i)

        def load_score(i):
            x = new_tile("score", i, [P, Q], BF16, bufs=5)
            nc.sync.dma_start(out=x[:], in_=score[i * P:(i + 1) * P, :])

        def load_vector_cols(cols, vector):
            nc.sync.dma_start(out=cols[:], in_=vector.rearrange("(h p t) -> p h t", h=2, t=4))

        def load_ref_high(h):
            rows = ref_high_words.rearrange("g p b -> p g b")[:, :, h * 2 * HALF:(h + 1) * 2 * HALF]
            nc.sync.dma_start(out=rh_words[h][:].bitcast(I32), in_=rows.bitcast(I32))

        def load_ref_low(h):
            x = new_tile("ref_raw", h, [P, 4, HALF], BF16)
            nc.sync.dma_start(out=x[:], in_=ref_low.rearrange("(p t) n -> p t n", t=4)[:, :, half_cols(h)])
            tiles["rows_raw", ("ref", h)] = x[:]

        def load_post(g):
            x = new_tile("post_raw", g, [P, 4, Q], BF16)
            nc.sync.dma_start(out=x[:], in_=post[g * GROUP:(g + 1) * GROUP, :].rearrange("(p t) n -> p t n", t=4))
            for h in range(2):
                tiles["rows_raw", ("post", g, h)] = x[:, :, half_cols(h)]

        def interleave_rows(key, copy):
            x = new_tile("rows_k", key, [P, 4 * HALF], BF16, bufs=3)
            copy(
                out=x[:].rearrange("p (c i t) -> p c t i", i=4, t=4),
                in_=tiles["rows_raw", key].rearrange("p t (c i) -> p c t i", i=4),
            )

        def quantize_rows(key):
            codes = new_tile("rows_codes", key, [P, HALF], U32, bufs=6)
            scales = new_tile("rows_scales", key, [P, HALF], U8, bufs=6)
            nc.vector.quantize_mx(out=codes[:].bitcast(FP8X4), scales=scales[:], in_=tiles["rows_k", key][:])

        def spread(name, cols):
            for h in range(2):
                bank = new_bank(name, h, [P, HALF])
                for t in range(4):
                    j = 4 * h + t
                    nc.tensor.transpose(bank[:, t * P:(t + 1) * P], cols[:, j:j + 1].to_broadcast([P, P]), ident[:])

        def pairs_out(copy, x, bank, groups):
            copy(out=x, in_=bank[:, 0:2 * groups, :].rearrange("p (g u) c -> p g c u", u=2))

        def as_pairs(x, groups):
            return x.bitcast(F32).rearrange("p (g c u) -> p g c u", g=groups, u=2)

        def turn_groups(kind, i, groups):
            words = tiles[kind, i][:].bitcast(F32)
            bank = new_bank(kind + "_turned", (i, groups[0]), [P, 4, P])
            for n, g in enumerate(groups):
                for u in range(2):
                    first = g * PAIRS + u * P
                    nc.tensor.transpose(bank[:, 2 * n + u, :], words[:, first:first + P], ident[:])
            return bank

        def cand_sort(i, kind, copy):
            groups = 4 if kind == "hi" else 1
            x = new_tile("cand_sorted_" + kind, i, [P, groups * PAIRS], F32)
            copy(
                out=x[:].rearrange("c (g u p) -> c g u p", g=groups, u=2),
                in_=tiles["cand_" + kind, i][:].bitcast(F32).rearrange("c (g p u) -> c g u p", g=groups, u=2),
            )

        def cand_turn(i):
            for kind, first_group, groups in (("hi", 0, 2), ("hi", 2, 2), ("lo", 0, 1)):
                bank = new_bank("cand_turned", (i, kind, first_group), [P, 4, P])
                for g in range(groups):
                    for u in range(2):
                        first = (first_group + g) * PAIRS
                        if i >= SORT_FROM:
                            src = tiles["cand_sorted_" + kind, i][:, first + P * u:first + P * (u + 1)]
                        else:
                            src = tiles["cand_" + kind, i][:].bitcast(F32)[:, first + u:first + PAIRS:2]
                        nc.tensor.transpose(bank[:, 2 * g + u, :], src, ident[:])
                if first_group == 0:
                    new_tile("cand_k_" + kind, i, [P, K2 if kind == "hi" else K1], BF16)
                x = tiles["cand_k_" + kind, i][:, first_group * GROUP:(first_group + groups) * GROUP]
                pairs_out(on_scalar, as_pairs(x, groups), bank, groups)

        def cand_quantize(i, kind):
            width = 4 * P if kind == "hi" else P
            step = 2 * P if kind == "hi" else P
            codes = new_tile("cand_codes_" + kind, i, [P, width], U32)
            scales = new_tile("cand_scales_" + kind, i, [P, width], U8)
            for first in range(0, width, step):
                nc.vector.quantize_mx(
                    out=codes[:, first:first + step].bitcast(FP8X4), scales=scales[:, first:first + step],
                    in_=tiles["cand_k_" + kind, i][:, 4 * first:4 * (first + step)],
                )

        def overlap(i, h):
            acc = new_bank("O", (i, h), [P, HALF])
            for g in range(K2 // GROUP):
                rows = slice(g * P, (g + 1) * P)
                nc.tensor.matmul_mx(
                    out=acc[:],
                    lhsT=tiles["cand_codes_hi", i][:, rows].bitcast(FP8X4),
                    lhsT_scale=tiles["cand_scales_hi", i][:, rows],
                    rhs=rh_words[h][:, g, :].bitcast(FP4X4),
                    rhs_scale=rh_scales[:, g, half_cols(h)],
                    start=(g == 0), stop=False,
                )
            nc.tensor.matmul_mx(
                out=acc[:],
                lhsT=tiles["cand_codes_lo", i][:].bitcast(FP8X4),
                lhsT_scale=tiles["cand_scales_lo", i][:],
                rhs=tiles["rows_codes", ("ref", h)][:].bitcast(FP8X4),
                rhs_scale=tiles["rows_scales", ("ref", h)][:],
                start=False, stop=True,
            )

        def length_share(i):
            x = new_tile("share", i, [P, R], F32)
            nc.scalar.activation(
                out=x[:], in_=ln_ref_len[:], func=ACT.Sigmoid, bias=ln_cand_len[:, i:i + 1], scale=-1.0,
            )

        def normalise(i, h):
            if h == 0:
                new_tile("S", i, [P, R], BF16)
            for u in range(2):
                cols = slice(h * HALF + u * 2 * P, h * HALF + (u + 1) * 2 * P)
                nc.vector.scalar_tensor_tensor(
                    out=tiles["S", i][:, cols].rearrange("c (p e) -> c p e", e=2),
                    in0=tiles["O", (i, h)][:].rearrange("c (p u e) -> c u p e", u=2, e=2)[:, u, :, :],
                    scalar=inv_cand_len[:, i:i + 1],
                    in1=tiles["share", i][:, cols].rearrange("c (p e) -> c p e", e=2),
                    op0=ALU.mult, op1=ALU.mult,
                )

        def s_turn(i, groups=(0, 1)):
            bank = turn_groups("S", i, groups)
            if groups[0] == 0:
                new_tile("S_k", i, [P, R], BF16, bufs=3)
            x = tiles["S_k", i][:, groups[0] * GROUP:(groups[-1] + 1) * GROUP]
            pairs_out(on_scalar, as_pairs(x, len(groups)), bank, len(groups))

        def s_quantize(i, groups=(0, 1)):
            if groups[0] == 0:
                new_tile("S_codes", i, [P, 2 * P], U32, bufs=4)
                new_tile("S_scales", i, [P, 2 * P], U8, bufs=4)
            rows = slice(groups[0] * P, (groups[-1] + 1) * P)
            nc.vector.quantize_mx(
                out=tiles["S_codes", i][:, rows].bitcast(FP8X4), scales=tiles["S_scales", i][:, rows],
                in_=tiles["S_k", i][:, groups[0] * GROUP:(groups[-1] + 1) * GROUP],
            )

        def expected(i, h, groups=(0, 1)):
            if groups[0] == 0:
                new_bank("U", (i, h), [P, HALF])
            for g in groups:
                rows = slice(g * P, (g + 1) * P)
                nc.tensor.matmul_mx(
                    out=tiles["U", (i, h)][:],
                    lhsT=tiles["S_codes", i][:, rows].bitcast(FP8X4),
                    lhsT_scale=tiles["S_scales", i][:, rows],
                    rhs=tiles["rows_codes", ("post", g, h)][:].bitcast(FP8X4),
                    rhs_scale=tiles["rows_scales", ("post", g, h)][:],
                    start=(g == 0), stop=(g == 1),
                )

        def apply_gain(i, h):
            if h == 0:
                new_tile("scaled", i, [P, Q], F32, bufs=3)
            nc.vector.tensor_tensor(
                out=tiles["scaled", i][:, half_cols(h)], in0=tiles["U", (i, h)][:], in1=gain_row[:, half_cols(h)],
                op=ALU.mult,
            )

        def second_stage(i):
            for h in range(2):
                expected(i, h)
            for h in range(2):
                apply_gain(i, h)

        def add_score(i, cols=slice(0, Q)):
            if cols.start == 0:
                new_tile("y", i, [P, Q], F32, bufs=4)
            y = tiles["y", i][:, cols]
            nc.vector.tensor_tensor(out=y, in0=tiles["scaled", i][:, cols], in1=tiles["score", i][:, cols], op=ALU.add)
            nc.sync.dma_start(out=out_0[i * P:(i + 1) * P, cols], in_=y)

        def y_round_group(i, g, copy):
            if g == 0:
                new_tile("Y", i, [P, Q], BF16, bufs=3)
            copy(
                out=tiles["Y", i][:, half_cols(g)].rearrange("c (u p e) -> c u p e", u=2, e=2),
                in_=tiles["y", i][:, half_cols(g)].rearrange("c (p u e) -> c u p e", u=2, e=2),
            )

        def on_gpsimd(out, in_):
            nc.gpsimd.tensor_scalar(out=out, in0=in_, scalar1=1.0, scalar2=0.0, op0=ALU.mult, op1=ALU.add)

        def y_round(i):
            if i in ROUND_ON_GPSIMD:
                for g in range(2):
                    y_round_group(i, g, on_gpsimd)
            else:
                x = new_tile("Y", i, [P, Q], BF16, bufs=3)
                on_scalar(
                    out=x[:].rearrange("c (g u p e) -> c g u p e", g=2, u=2, e=2),
                    in_=tiles["y", i][:].rearrange("c (g p u e) -> c g u p e", g=2, u=2, e=2),
                )

        def y_turn(i, groups=(0, 1), copy=on_scalar):
            bank = turn_groups("Y", i, groups)
            if i % 2 == 0:
                new_tile("Y_k", i // 2, [P, 2, 2 * 4 * P], BF16, bufs=3)
            x = tiles["Y_k", i // 2][:, groups[0]:groups[-1] + 1, (i % 2) * 4 * P:(i % 2 + 1) * 4 * P]
            pairs_out(copy, x.bitcast(F32).rearrange("p g (c u) -> p g c u", u=2), bank, len(groups))

        words_out = out_1.rearrange("g p m t -> p g (m t)").bitcast(I32)
        scales_out = out_2.rearrange("g q m -> q g m").bitcast(I32)

        def y_quantize(couple, g):
            if g == 0:
                new_tile("y_codes", couple, [P, 2, 2 * P], U32, bufs=3)
            rows = slice(couple * 2 * P, (couple + 1) * 2 * P)
            codes = tiles["y_codes", couple]
            nc.vector.quantize_mx(
                out=codes[:, g, :].bitcast(FP8X4), scales=y_scales[:, g, rows], in_=tiles["Y_k", couple][:, g, :],
            )
            if couple == LAST // 2:
                nc.sync.dma_start(out=words_out[:, g, rows], in_=codes[:, g, :].bitcast(I32))
            elif g == 1:
                nc.sync.dma_start(out=words_out[:, :, rows], in_=codes[:].bitcast(I32))

        nc.vector.memset(rh_scales[:].rearrange("p g n -> p (g n)").bitcast(I32), 0)
        nc.vector.memset(len_square[:], 1.0)
        make_identity(nc, ident[:])

        load_cand_part("hi", 0)
        load_vector_cols(ref_len_cols, ref_len)
        nc.sync.dma_start(out=len_rows[:], in_=cand_len.rearrange("(i p) -> i p", p=P))
        load_cand_part("lo", 0)
        load_ref_low(0)
        load_ref_high(0)
        scale_rows = ref_high_scales.rearrange("g q n -> q g n").bitcast(I32)
        for quad in range(4):
            nc.sync.dma_start(
                out=rh_scales[32 * quad:32 * quad + 4, :, :].bitcast(I32), in_=scale_rows[4 * quad:4 * quad + 4, :, :],
            )
        load_vector_cols(gain_cols, gain)
        load_ref_low(1)
        load_cand(1)
        load_ref_high(1)
        load_post(0)
        load_cand(2)
        load_post(1)
        load_cand(3)

        nc.scalar.activation(out=ln_ref_len_cols[:], in_=ref_len_cols[:].rearrange("p h t -> p (h t)"), func=ACT.Ln)
        on_vector(out=len_square[0:TILES, :], in_=len_rows[:])
        cand_turn(0)
        len_turned = new_bank("len_turned", 0, [P, 4, P])
        nc.tensor.transpose(len_turned[:, 0, :], len_square[:], ident[:])
        spread("ln_ref_len_turned", ln_ref_len_cols)
        nc.scalar.activation(out=ln_cand_len[:], in_=len_turned[:, 0, 0:TILES], func=ACT.Ln)
        interleave_rows(("ref", 0), on_vector)
        cand_quantize(0, "hi")
        quantize_rows(("ref", 0))
        cand_quantize(0, "lo")
        nc.vector.reciprocal(out=inv_cand_len[:], in_=len_turned[:, 0, 0:TILES])
        for h in range(2):
            on_scalar(
                out=ln_ref_len[:, half_cols(h)].rearrange("c (u p e) -> c u p e", u=2, e=2),
                in_=tiles["ln_ref_len_turned", h][:].rearrange("c (u e p) -> c u p e", u=2, e=2),
            )
        length_share(0)
        on_vector(out=gain_cols_f32[:], in_=gain_cols[:].rearrange("p h t -> p (h t)"))
        overlap(0, 0)
        spread("gain_turned", gain_cols_f32)
        for h in range(2):
            on_scalar(
                out=gain_row[:, half_cols(h)].rearrange("c (p t) -> c p t", t=4),
                in_=tiles["gain_turned", h][:].rearrange("c (t p) -> c p t", t=4),
            )
        interleave_rows(("ref", 1), on_vector)
        normalise(0, 0)
        quantize_rows(("ref", 1))

        for n in range(LAST):
            if n >= 1:
                load_score(n - 1)
            if n == LAST - 1:
                load_score(LAST - 1)
                load_score(LAST)
            if n + 4 <= LAST:
                load_cand(n + 4)

            if n >= 1:
                s_turn(n - 1)
            cand_turn(n + 1)
            if n >= 4:
                y_turn(n - 4)
            if n == 1:
                quantize_rows(("post", 0, 1))
            if n == 2:
                quantize_rows(("post", 1, 1))
            if n >= 1:
                s_quantize(n - 1)
            if n >= 6:
                y_quantize((n - 6) // 2, n % 2)
            sort_ahead = SORT_FROM <= n + 2 <= LAST
            if sort_ahead:
                cand_sort(n + 2, "lo", on_vector)
            cand_quantize(n + 1, "hi")
            cand_quantize(n + 1, "lo")
            length_share(n + 1)
            if sort_ahead:
                cand_sort(n + 2, "hi", on_scalar)
            if n == 3:
                y_round(0)
            if n >= 3:
                add_score(n - 2)
                y_round(n - 2)

            overlap(n, 1)
            normalise(n, 1)
            if n == 0:
                interleave_rows(("post", 0, 0), on_vector)
                interleave_rows(("post", 0, 1), on_scalar)
            if n == 1:
                interleave_rows(("post", 1, 1), on_scalar)
                interleave_rows(("post", 1, 0), on_vector)
            if n == 2:
                second_stage(0)
            if n >= 2:
                second_stage(n - 1)
            overlap(n + 1, 0)
            if n == 2:
                add_score(0)
            normalise(n + 1, 0)
            if n <= 1:
                quantize_rows(("post", n, 0))

        s_turn(LAST - 1)
        y_turn(LAST - 4)
        y_quantize(1, 1)
        s_quantize(LAST - 1)
        add_score(LAST - 2)
        overlap(LAST, 1)
        s_turn(LAST, (0,))
        y_round(LAST - 2)
        normalise(LAST, 1)
        for h in range(2):
            expected(LAST - 1, h)
        s_quantize(LAST, (0,))
        for h in range(2):
            apply_gain(LAST - 1, h)
        s_turn(LAST, (1,))
        y_turn(LAST - 3)
        for h in range(2):
            expected(LAST, h, (0,))
        y_turn(LAST - 2)
        s_quantize(LAST, (1,))
        add_score(LAST - 1)
        y_round(LAST - 1)
        for h in range(2):
            expected(LAST, h, (1,))
        for h in range(2):
            apply_gain(LAST, h)
        for h in range(2):
            add_score(LAST, half_cols(h))
        y_round_group(LAST, 0, on_scalar)
        y_quantize(2, 0)
        y_round_group(LAST, 1, on_vector)
        y_quantize(2, 1)
        y_quantize(3, 0)
        y_turn(LAST - 1)
        y_turn(LAST, (0,), on_scalar)
        y_quantize(3, 1)
        y_turn(LAST, (1,), on_vector)
        y_quantize(4, 0)
        y_quantize(4, 1)
        for quad in range(4):
            nc.sync.dma_start(
                out=scales_out[4 * quad:4 * quad + 4, :, :], in_=y_scales[32 * quad:32 * quad + 4, :, :].bitcast(I32),
            )
